import numpy as np, ml_dtypes
CORES = [48,51,52,55]
N = 4
BF = ml_dtypes.bfloat16
def f(rng, *shape):
    return (rng.standard_normal(shape, dtype=np.float32) * np.exp2(rng.integers(-2, 3, shape[:-1] + (1,)))).astype(BF)
def wide(rng, *shape):
    v = f(rng, *shape).astype(np.float32); k = shape[:-2] + (1, shape[-1])
    return (v * np.exp2(rng.integers(-6, 7, k)) * (rng.random(k) > 0.0625)).astype(BF)
def gentries(a):
    return np.ascontiguousarray(a.reshape(8, 16, -1).transpose(0, 2, 1)).reshape(8, -1)
def gtable(e):
    e = np.asarray(e); return np.ascontiguousarray(e.reshape(8, -1, 16).transpose(0, 2, 1)).reshape(128, -1).astype(np.int32)
W, F, U, CAP, SW = 3, 256, 4, 32, 3
C = W * F; Z = C + (W - 1) * N * CAP
def pack(x):
    return np.stack([gtable(v.reshape(8, -1)) for v in x])
def unpack(x):
    return np.stack([gentries(v) for v in x])
def sends(rng, full):
    x = np.argsort(rng.random((N, 8, W - 1, N, F)), axis=-1)[..., :CAP] + F * np.arange(W - 1).reshape(1, 1, W - 1, 1, 1)
    n = rng.integers(0, CAP + 1, (N, 8, W - 1, N, 1)); n[0, :, 0, 1] = CAP
    if full: n[:] = CAP
    keep = (np.argsort(rng.random(x.shape), axis=-1) < n) & (np.arange(N).reshape(N, 1, 1, 1, 1) != np.arange(N).reshape(1, 1, 1, N, 1))
    return np.where(keep, x, Z)
def upwind(rng, far, none):
    s = (N, 8, W, U, F); r = np.arange(N).reshape(N, 1, 1, 1, 1); w = np.arange(W).reshape(1, 1, W, 1, 1)
    v = np.where(rng.random(s) < 0.75, w - 1, (rng.random(s) * w).astype(np.int64))
    near = v * F + rng.integers(0, F, s); away = C + (v * N + (r + 1 + rng.integers(0, N - 1, s)) % N) * CAP + rng.integers(0, CAP, s)
    p = rng.random(s)
    return np.where(w == 0, Z, np.where(p < far, away, np.where(p < far + none, Z, near)))
def draw(rng, o, p, x):
    return {"qs": f(rng, N, 128, C), "rm": (0.5 + 0.5 * rng.random((N, 128, C))).astype(BF), "co": (0.75 * rng.random((N, 128, U * C))).astype(BF),
            "sc": (f(rng, N, 16, 16).astype(np.float32) * np.float32(0.0625)).astype(BF), "seq": pack(o), "up": pack(p), "snd": pack(x)}
def orders(rng):
    return np.argsort(rng.random((N, 8, C)), axis=-1)
def setup_inputs(rng):
    return draw(rng, orders(rng), upwind(rng, 0.5, 0.1), sends(rng, False))
def setup_inputs_full(rng):
    return draw(rng, orders(rng), upwind(rng, 0.9, 0.0), sends(rng, True))
def setup_inputs_chain(rng):
    w = np.arange(W).reshape(1, 1, W, 1, 1); r = np.arange(N).reshape(N, 1, 1, 1, 1); x = sends(rng, True)
    p = np.where(w == 0, Z, C + ((w - 1) * N + (r + 1) % N) * CAP + rng.integers(0, CAP, (N, 8, W, U, F)))
    other = np.arange(N).reshape(N, 1, 1, 1) != np.arange(N).reshape(1, 1, 1, N); a = F * np.arange(W - 1).reshape(1, 1, W - 1, 1)
    x[..., 0] = np.where(other, a, Z); x[..., CAP - 1] = np.where(other, a + F - 1, Z)
    return draw(rng, orders(rng), p, x)
def setup_inputs_alike(rng):
    x = sends(rng, True); x[:] = x[..., :1].copy(); p = upwind(rng, 0.5, 0.1); p = np.repeat(p[:, :, :, :1], U, axis=3)
    o = orders(rng); o[:, 0] = np.arange(C); o[:, 1] = np.arange(C)[::-1]; o[:, 3] = o[:, 2]
    return draw(rng, o, p, x)
def setup_inputs_few(rng):
    x = sends(rng, False); k = int(rng.integers(0, N)); x[k] = Z; x[:, :, :, k] = Z
    d = draw(rng, orders(rng), upwind(rng, 0.08, 0.85), x); d["rm"] = np.where(rng.random(d["rm"].shape) < 0.125, np.float32(0), d["rm"].astype(np.float32)).astype(BF)
    return d
def setup_inputs_spread(rng):
    d = setup_inputs(rng); d["qs"] = wide(rng, N, 128, C); return d
def check_inputs(d):
    bad = []
    if not (np.sort(unpack(d["seq"]), axis=-1) == np.arange(C)).all(): bad.append("seq")
    p = unpack(d["up"]).reshape(N, 8, W, U * F).astype(np.int64); w = np.arange(W).reshape(1, 1, W, 1); r = np.arange(N).reshape(N, 1, 1, 1); s = p - C
    if not ((p == Z) | ((p >= 0) & (p < w * F)) | ((s >= 0) & (s < w * N * CAP) & ((s // CAP) % N != r))).all(): bad.append("up")
    x = unpack(d["snd"]).reshape(N, 8, W - 1, N, CAP).astype(np.int64); w = np.arange(W - 1).reshape(1, 1, W - 1, 1, 1)
    other = np.arange(N).reshape(N, 1, 1, 1, 1) != np.arange(N).reshape(1, 1, 1, N, 1)
    if not ((x == Z) | ((x >= w * F) & (x < w * F + F) & other)).all(): bad.append("snd")
    if not all(np.isfinite(d[k].astype(np.float32)).all() for k in ("qs", "rm", "co", "sc")): bad.append("finite")
    return bad
def reference(qs, rm, co, sc, seq, up, snd):
    o = unpack(seq).astype(np.int64); p = unpack(up).astype(np.int64); x = unpack(snd).astype(np.int64)
    src = qs.astype(np.float64).reshape(N, 8, 16, C); rem = rm.astype(np.float64).reshape(N, 8, 16, C); a = co.astype(np.float64).reshape(N, 8, 16, W, U, F)
    s = sc.astype(np.float64).transpose(0, 2, 1); y = np.zeros((N, 16, C), np.float64)
    for k in range(SW):
        win = np.zeros((N, 8, 16, Z + 1), np.float64)
        for w in range(W):
            c = o[:, :, None, w * F:w * F + F]
            h = np.take_along_axis(win, p[:, :, None, w * U * F:(w + 1) * U * F], 3).reshape(N, 8, 16, U, F)
            v = (np.take_along_axis(src, c, 3) + np.sum(a[:, :, :, w] * h, axis=3)) * np.take_along_axis(rem, c, 3)
            win[..., w * F:w * F + F] = v
            if w == W - 1: continue
            for r in range(N):
                for q in range(N):
                    if q == r: continue
                    b = C + (w * N + r) * CAP; e = (w * N + q) * CAP
                    win[q, :, :, b:b + CAP] = np.take_along_axis(win[r], x[r][:, None, e:e + CAP], 2)
        psi = np.zeros((N, 8, 16, C), np.float64); np.put_along_axis(psi, o[:, :, None], win[..., :C], 3)
        flux = np.sum(psi, axis=1); y = y + flux
        src = np.repeat(np.matmul(s, flux)[:, None], 8, axis=1)
    return {"y": y.astype(np.float32)}

@@ -1,0 +1,321 @@
+from concourse.bass import DstId, RemoteDMATransfer
+from concourse.mybir import AluOpType, ActivationFunctionType
+
+F, SW = 256, 3
+ZC = 512
+ST = 257
+SL = 768
+CH = [(0, 320), (320, 576), (576, 768)]
+
+SCRATCH = {
+    "seqi": ("sbuf", [128, 48], "int32"), "upi": ("sbuf", [128, 128], "int32"), "sndi": ("sbuf", [128, 16], "int32"),
+    "upt": ("sbuf", [128, 128], "int32"), "upz": ("sbuf", [128, 128], "int32"),
+    "seq16": ("sbuf", [128, 48], "uint16"), "up16": ("sbuf", [128, 128], "uint16"), "sa16": ("sbuf", [128, 12], "uint16"),
+    "lst2": ("sbuf", [128, 30], "uint16"), "cmp16": ("sbuf", [128, 30], "uint16"),
+    "qsb": ("sbuf", [128, 768], "bfloat16"), "rmb": ("sbuf", [128, 768], "bfloat16"), "cob": ("sbuf", [128, 2048], "bfloat16"),
+    "scb": ("sbuf", [128, 16], "bfloat16"), "oneb": ("sbuf", [128, 480], "bfloat16"), "e2": ("sbuf", [128, 480], "bfloat16"),
+    "onef": ("sbuf", [128, 128], "float32"), "idn": ("sbuf", [128, 128], "float32"), "sct": ("sbuf", [128, 128], "float32"),
+    "msk": ("sbuf", [128, 480], "float32"), "iot": ("sbuf", [128, 1024], "float32"),
+    "win0": ("sbuf", [128, 1024], "float32"), "win1": ("sbuf", [128, 1024], "float32"),
+    "c1": ("sbuf", [128, 5 * ST + 3], "float32"), "c2": ("sbuf", [128, 1024], "float32"), "row": ("sbuf", [128, 5 * ST + 3], "float32"),
+    "rmp": ("sbuf", [128, 512], "float32"), "ks": ("sbuf", [128, 480], "float32"), "mg": ("sbuf", [128, 480], "float32"),
+    "sp1": ("sbuf", [128, 264], "float32"), "sp2": ("sbuf", [128, 256], "float32"), "sps": ("sbuf", [128, 96], "float32"),
+    "src": ("sbuf", [128, 776], "float32"),
+    "pr1": ("sbuf", [128, 1024], "float32"), "pr2": ("sbuf", [128, 1024], "float32"), "prs": ("sbuf", [128, 384], "float32"),
+    "b1": ("sbuf", [128, 256], "float32"), "b2": ("sbuf", [128, 256], "float32"), "bs": ("sbuf", [128, 96], "float32"),
+    "cb0": ("sbuf", [128, 768], "float32"), "cb1": ("sbuf", [128, 768], "float32"), "cb2": ("sbuf", [128, 768], "float32"),
+    "ysb": ("sbuf", [128, 768], "float32"),
+    "sb0": ("sbuf", [128, 96], "float32"), "sb1": ("sbuf", [128, 96], "float32"), "sb2": ("sbuf", [128, 96], "float32"),
+    "sb3": ("sbuf", [128, 96], "float32"), "sb4": ("sbuf", [128, 96], "float32"), "sb5": ("sbuf", [128, 96], "float32"),
+    "ps_s0": ("psum", [128, 512], "float32"), "ps_s1": ("psum", [128, 512], "float32"), "ps_s2": ("psum", [128, 512], "float32"),
+    "ps_y0": ("psum", [128, 512], "float32"), "ps_y1": ("psum", [128, 512], "float32"), "ps_w1": ("psum", [128, 512], "float32"),
+    "ps_w2": ("psum", [128, 512], "float32"), "ps_c": ("psum", [128, 512], "float32"),
+}
+LOADS = ["seqi", "upi", "sndi", "qsb", "rmb", "co1", "co2", "scb"]
+SEMAPHORES = (["q_v", "q_a", "q_p", "q_g", "sent", "y0", "y1"] + ["ld_" + n for n in LOADS] + ["arr%d" % i for i in range(6)])
+
+
+def plan(src, cores, topo):
+    dst = [c for c in cores if c != src]
+    far = [c for c in dst if topo.die(c) != topo.die(src)]
+    near = [c for c in dst if topo.die(c) == topo.die(src)]
+    res = {}
+    for group, first in ((far, 0), (near, 1)):
+        for i, d in enumerate(group):
+            e = topo.engines(src, d)[first::2]
+            n = len(e) // len(group)
+            res[d] = e[i * n:(i + 1) * n]
+    return res
+
+
+def rank_program(g, core, T, topo):
+    rank = T.rank_of(core)
+    if rank is None:
+        return
+    A = AluOpType
+    COPY = ActivationFunctionType.Copy
+    cores = list(T.cores)
+    others = [d for d in range(len(cores)) if d != rank]
+    eng = {"v": g.vector, "a": g.scalar, "p": g.tensor, "g": g, "s": g.sync}
+
+    count, hist, clock = {}, {}, {}
+    known = {q: {} for q in eng}
+
+    def need(q, tok):
+        s, c = tok
+        if known[q].get(s, 0) >= c:
+            return
+        eng[q].wait_ge(T.sem[s], c)
+        for s2, c2 in clock.get(tok, {}).items():
+            if known[q].get(s2, 0) < c2:
+                known[q][s2] = c2
+        known[q][s] = c
+
+    def deps(q, reads, writes):
+        toks = {}
+        for lst, w in ((reads, True), (writes, False)):
+            for x in lst:
+                n, lo, hi = x[:3]
+                psum = n[:3] == "ps_"
+                for (l2, h2, kind, tok, q2) in hist.get(n, []):
+                    if psum:
+                        hit = q2 != q
+                    else:
+                        hit = l2 < hi and lo < h2 and (kind == "w" or not w)
+                    if hit and toks.get(tok[0], 0) < tok[1]:
+                        toks[tok[0]] = tok[1]
+        for s in sorted(toks, key=lambda s: -len(clock.get((s, toks[s]), {}))):
+            need(q, (s, toks[s]))
+
+    def note(q, reads, writes, tok):
+        for lst, kind in ((reads, "r"), (writes, "w")):
+            for x in lst:
+                h = hist.setdefault(x[0], [])
+                if kind == "w" and x[0][:3] != "ps_":
+                    h[:] = [e for e in h if not (x[1] <= e[0] and e[1] <= x[2])]
+                h.append((x[1], x[2], kind, tok, q))
+
+    def emit(q, fn, reads, writes, sem=None, n=1):
+        deps(q, reads, writes)
+        s = sem or "q_" + q
+        count[s] = count.get(s, 0) + n
+        fn().then_inc(T.sem[s], n)
+        tok = (s, count[s])
+        c = dict(known[q])
+        c[s] = count[s]
+        clock[tok] = c
+        note(q, reads, writes, tok)
+
+    def ap(x):
+        p = x[3] if len(x) > 3 else 128
+        return T[x[0]][0:p, x[1]:x[2]]
+
+    def ind(w, o):
+        return T[w[0]][:, w[1]:w[2]].indirect(T[o[0]][:, o[1]:o[2]])
+
+    def load(q, sem, dst, src_ap):
+        emit(q, lambda: eng[q].dma_start(ap(dst), src_ap), [], [dst], sem="ld_" + sem, n=16)
+
+    def fill(x, v, ap_=None):
+        emit("v", lambda: g.vector.memset(ap_ if ap_ is not None else ap(x), v), [], [x])
+
+    def tt(out, a, b, op):
+        emit("v", lambda: g.vector.tensor_tensor(ap(out), ap(a), ap(b), op), [a, b], [out])
+
+    def gtt(out, w, o, b):
+        emit("v", lambda: g.vector.tensor_tensor(ap(out), ind(w, o), ap(b), A.mult), [w, o, b], [out])
+
+    def gv(out, w, o):
+        emit("v", lambda: g.vector.tensor_copy(ap(out), ind(w, o)), [w, o], [out])
+
+    def ga(out, w, o):
+        emit("a", lambda: g.scalar.activation(ap(out), ind(w, o), COPY), [w, o], [out])
+
+    def cpv(out, a):
+        emit("v", lambda: g.vector.tensor_copy(ap(out), ap(a)), [a], [out])
+
+    def cpa(out, a):
+        emit("a", lambda: g.scalar.activation(ap(out), ap(a), COPY), [a], [out])
+
+    def ts(out, a, s1, s2, op0, op1=None):
+        if op1 is None:
+            emit("v", lambda: g.vector.tensor_scalar(ap(out), ap(a), s1, None, op0), [a], [out])
+        else:
+            emit("v", lambda: g.vector.tensor_scalar(ap(out), ap(a), s1, s2, op0, op1), [a], [out])
+
+    def mm(out, l, r, start, stop, rhs=None):
+        emit("p", lambda: g.tensor.matmul(ap(out), ap(l), rhs if rhs is not None else ap(r), start, stop), [l, r], [out])
+
+    IDN = ("idn", 0, 128)
+
+    def scatter_copy(cb, w, a):
+        o = ("seq16", 16 * w, 16 * w + 16)
+        emit("v", lambda: g.vector.tensor_copy(ind((cb, 0, 768), o), ap(a)), [o, a], [(cb, 0, 768)])
+
+    myplan = plan(core, cores, topo)
+
+    def send(k, w):
+        i = 2 * k + w
+        sb = "sb%d" % i
+        deps("g", [(sb, 0, 96)], [])
+        tr = []
+        lo = SL + (w * len(cores) + rank) * 32
+        for j, d in enumerate(others):
+            rid, pid = topo.addr(cores[d])[:2]
+            m = 0
+            for e in myplan[cores[d]]:
+                m |= 1 << e
+            tr.append(RemoteDMATransfer(dst_ids=[DstId(rid=rid, pnc=pid)], dma_engine_mask=m, remote_sem=T.sem["arr%d" % i],
+                                        src=T[sb][:, 32 * j:32 * j + 32], dst=T["win%d" % (k % 2)][:, lo:lo + 32]))
+            count["sent"] = count.get("sent", 0) + len(myplan[cores[d]])
+        g.remote_dma_fused(tr, local_sem=T.sem.sent)
+        tot = sum(len(plan(cores[d], cores, topo)[core]) for d in others)
+        for d in others:
+            a = SL + (w * len(cores) + d) * 32
+            note("net", [], [("win%d" % (k % 2), a, a + 32)], ("arr%d" % i, tot))
+
+    load("s", "seqi", ("seqi", 0, 48), T.seq[:, :])
+    load("a", "qsb", ("qsb", 0, 768), T.qs[:, :])
+    load("s", "rmb", ("rmb", 0, 768), T.rm[:, :])
+    load("a", "sndi", ("sndi", 0, 16), T.snd[:, :])
+    load("s", "upi", ("upi", 0, 128), T.up[:, 64:192])
+    load("s", "co1", ("cob", 0, 1024), T.co[:, 1024:2048])
+    load("a", "co2", ("cob", 1024, 2048), T.co[:, 2048:3072])
+    load("s", "scb", ("scb", 0, 16, 16), T.sc[:, :])
+
+    fill(("onef", 0, 128), 1.0)
+    fill(("oneb", 0, 480, 16), 1.0)
+    emit("g", lambda: g.affine_select(T.idn[:, :], T.onef[:, :], [[-1, 128]], A.is_equal, 0.0, 0, 1), [("onef", 0, 128)], [IDN])
+    emit("g", lambda: g.affine_select(T.e2[0:16, :], T.oneb[0:16, :], [[0, 30], [1, 16]], A.is_equal, 0.0, 0, -1),
+         [("oneb", 0, 480)], [("e2", 0, 480)])
+    for b in ("win0", "win1"):
+        fill((b, 256, SL), 0.0)
+        for w in (0, 1):
+            lo = SL + (w * len(cores) + rank) * 32
+            fill((b, lo, lo + 32), 0.0)
+    fill(("c1", 0, 5 * ST), 0.0, T.c1[:, 256:5 * ST:ST])
+    fill(("row", 0, 4 * ST), float(ZC), T.row[:, 256:4 * ST:ST])
+    fill(("row", 5 * ST - 1, 5 * ST), 768.0)
+    fill(("sp1", 256, 264), 0.0)
+    fill(("src", 768, 776), 0.0)
+
+    RM0 = ("c1", 4 * ST, 4 * ST + 256)
+    SEQ = [("seq16", 16 * w, 16 * w + 16) for w in range(3)]
+    cpv(("seq16", 0, 48), ("seqi", 0, 48))
+
+    def snd_list(w):
+        j = 0
+        while j < 3:
+            n = 1
+            while j + n < 3 and others[j + n] == others[j] + n:
+                n += 1
+            a = 8 * w + 2 * others[j]
+            ts(("sa16", 6 * w + 2 * j, 6 * w + 2 * (j + n)), ("sndi", a, a + 2 * n), float(ZC), None, A.min)
+            j += n
+
+    snd_list(0)
+    ga(RM0, ("rmb", 0, 768), SEQ[0])
+    gtt(("win0", 0, 256), ("qsb", 0, 768), SEQ[0], RM0)
+    gv(("sb0", 0, 96), ("win0", 0, 520), ("sa16", 0, 6))
+    send(0, 0)
+    emit("g", lambda: g.iota(T.iot[:, :], [[1, 1024]], 0, 0, allow_small_or_imprecise_dtypes=True), [], [("iot", 0, 1024)])
+
+    RMP = [("rmp", 0, 256), ("rmp", 256, 512)]
+    PRM = [("ps_c", 0, 256), ("ps_s2", 0, 256)]
+    for w in (0, 1):
+        ga(RMP[w], ("rmb", 0, 768), SEQ[w + 1])
+        cpa(PRM[w], RMP[w])
+    mm(("ps_s0", 0, 480), ("e2", 0, 128, 16), ("e2", 0, 480, 16), True, True)
+    for o in range(8):
+        mm(("ps_s1", 16 * o, 16 * o + 16), ("e2", 0, 128, 16), ("scb", 0, 16, 16), True, True)
+    ts(("upt", 0, 128), ("upi", 0, 128), 1024.0, float(ZC - 1024), A.is_equal, A.mult)
+    tt(("upz", 0, 128), ("upi", 0, 128), ("upt", 0, 128), A.add)
+    cpv(("up16", 0, 128), ("upz", 0, 128))
+    gtt(("sp1", 0, 256), ("qsb", 0, 768), SEQ[1], RMP[0])
+    mm(("ps_w1", 0, 256), IDN, ("sp1", 0, 256), True, False)
+    for u in range(4):
+        tt(("c1", ST * u, ST * u + 256), ("cob", 256 * u, 256 * u + 256), PRM[0], A.mult)
+    gtt(("sp2", 0, 256), ("qsb", 0, 768), SEQ[2], RMP[1])
+    mm(("ps_w2", 0, 256), IDN, ("sp2", 0, 256), True, False)
+    for u in range(4):
+        tt(("c2", 256 * u, 256 * u + 256), ("cob", 1024 + 256 * u, 1280 + 256 * u), PRM[1], A.mult)
+    snd_list(1)
+    cpa(("msk", 0, 480), ("ps_s0", 0, 480))
+    cpa(("sct", 0, 128), ("ps_s1", 0, 128))
+    for u in range(4):
+        ga(("row", ST * u, ST * u + 256), ("iot", 0, 1024), ("up16", 16 * u, 16 * u + 16))
+    ga(("row", ST * 4, ST * 4 + 256), ("iot", 0, 1024), SEQ[0])
+
+    def psi1(b):
+        for u in range(4):
+            gtt(("pr1", 256 * u, 256 * u + 256), (b, 0, 896), ("up16", 16 * u, 16 * u + 16), ("c1", ST * u, ST * u + 256))
+            if u < 2:
+                mm(("ps_w1", 0, 256), IDN, ("pr1", 256 * u, 256 * u + 256), False, u == 1)
+        tt(("b1", 0, 256), ("pr1", 512, 768), ("ps_w1", 0, 256), A.add)
+        tt((b, 256, 512), ("b1", 0, 256), ("pr1", 768, 1024), A.add)
+
+    def psi2(b, cb):
+        for u, n in ((0, 1), (1, 1), (2, 2)):
+            c = (256 * u, 256 * (u + n))
+            gtt(("pr2",) + c, (b, 0, 1024), ("up16", 64 + 16 * u, 64 + 16 * (u + n)), ("c2",) + c)
+            if u < 2:
+                mm(("ps_w2", 0, 256), IDN, ("pr2",) + c, False, u == 1)
+        tt(("b2", 0, 256), ("pr2", 512, 768), ("ps_w2", 0, 256), A.add)
+        x, y, o = ("b2", 0, 256), ("pr2", 768, 1024), SEQ[2]
+        emit("v", lambda: g.vector.tensor_tensor(ind((cb, 0, 768), o), ap(x), ap(y), A.add), [x, y, o], [(cb, 0, 768)])
+
+    def flux(k):
+        for h in (0, 1):
+            mm(("ps_y%d" % h, 0, 384, 16), ("msk", 0, 16), ("cb%d" % k, 384 * h, 384 * h + 384), k == 0, k == SW - 1)
+
+    psi1("win0")
+    gv(("sb1", 0, 96), ("win0", 0, 520), ("sa16", 6, 12))
+    send(0, 1)
+    scatter_copy("cb0", 0, ("win0", 0, 256))
+    for u in range(4):
+        ts(("lst2", 6 * u, 6 * u + 6), ("sa16", 6, 12), float(ST * u - 256), None, A.add)
+    ts(("lst2", 24, 30), ("sa16", 0, 6), 256.0, float(4 * ST), A.min, A.add)
+    gtt(("mg", 0, 480), ("row", 0, 5 * ST), ("lst2", 0, 30), ("msk", 0, 480))
+    for j in range(16):
+        mm(("ps_s1", 0, 30), IDN, ("mg", 0, 480), j == 0, j == 15, rhs=T.mg[:, j:480:16])
+    ga(("ks", 0, 480), ("c1", 0, 5 * ST), ("lst2", 0, 30))
+    scatter_copy("cb0", 1, ("win0", 256, 512))
+    cpv(("cmp16", 0, 30), ("ps_s1", 0, 30))
+    psi2("win0", "cb0")
+
+    for k in range(1, SW):
+        b, cb = "win%d" % (k % 2), "cb%d" % k
+        for i, (lo, hi) in enumerate(CH):
+            p = ("ps_s%d" % i, 0, hi - lo)
+            mm(p, ("sct", 0, 128), ("cb%d" % (k - 1), lo, hi), True, True)
+            (cpa if i == 1 else cpv)(("src", lo, hi), p)
+        gtt(("sb%d" % (2 * k), 0, 96), ("src", 0, 769), ("cmp16", 24, 30), ("ks", 384, 480))
+        send(k, 0)
+        gtt(("sp1", 0, 256), ("src", 0, 769), SEQ[1], RMP[0])
+        gv(("sps", 0, 96), ("sp1", 0, 257), ("lst2", 0, 6))
+        mm(("ps_c", 0, 96), IDN, ("sps", 0, 96), True, False)
+        gtt((b, 0, 256), ("src", 0, 769), SEQ[0], RM0)
+        mm(("ps_w1", 0, 256), IDN, ("sp1", 0, 256), True, False)
+        gtt(("sp2", 0, 256), ("src", 0, 769), SEQ[2], RMP[1])
+        mm(("ps_w2", 0, 256), IDN, ("sp2", 0, 256), True, False)
+        scatter_copy(cb, 0, (b, 0, 256))
+        for u, n in ((0, 1), (1, 1), (2, 2)):
+            c = (96 * u, 96 * (u + n))
+            gtt(("prs",) + c, (b, 0, 896), ("cmp16", 6 * u, 6 * (u + n)), ("ks",) + c)
+            if u < 2:
+                mm(("ps_c", 0, 96), IDN, ("prs",) + c, False, u == 1)
+        tt(("bs", 0, 96), ("prs", 192, 288), ("ps_c", 0, 96), A.add)
+        tt(("sb%d" % (2 * k + 1), 0, 96), ("bs", 0, 96), ("prs", 288, 384), A.add)
+        send(k, 1)
+        psi1(b)
+        scatter_copy(cb, 1, (b, 256, 512))
+        flux(k - 1)
+        psi2(b, cb)
+    flux(SW - 1)
+
+    for h, cp, q in ((0, cpv, "s"), (1, cpa, "a")):
+        x = ("ysb", 384 * h, 384 * h + 384, 16)
+        cp(x, ("ps_y%d" % h, 0, 384, 16))
+        emit(q, lambda: eng[q].dma_start(T.y[:, 384 * h:384 * h + 384], ap(x)), [x], [], sem="y%d" % h, n=16)
+    for s in ("q_v", "q_a", "q_p", "q_g", "y0", "y1", "sent"):
+        g.wait_ge(T.sem[s], count[s])

@@ -1,36 +1,25 @@
 from concourse.bass import DstId, RemoteDMATransfer
 from concourse.mybir import AluOpType, ActivationFunctionType
 
-F, SW = 256, 3
+SW = 3
 ZC = 512
-ST = 257
 SL = 768
-CH = [(0, 320), (320, 576), (576, 768)]
+CH = [(0, 320), (320, 592), (592, 768)]
+YC = [(0, 512), (512, 768)]
+F32, BF, I32, U16 = "float32", "bfloat16", "int32", "uint16"
 
-SCRATCH = {
-    "seqi": ("sbuf", [128, 48], "int32"), "upi": ("sbuf", [128, 128], "int32"), "sndi": ("sbuf", [128, 16], "int32"),
-    "upt": ("sbuf", [128, 128], "int32"), "upz": ("sbuf", [128, 128], "int32"),
-    "seq16": ("sbuf", [128, 48], "uint16"), "up16": ("sbuf", [128, 128], "uint16"), "sa16": ("sbuf", [128, 12], "uint16"),
-    "lst2": ("sbuf", [128, 30], "uint16"), "cmp16": ("sbuf", [128, 30], "uint16"),
-    "qsb": ("sbuf", [128, 768], "bfloat16"), "rmb": ("sbuf", [128, 768], "bfloat16"), "cob": ("sbuf", [128, 2048], "bfloat16"),
-    "scb": ("sbuf", [128, 16], "bfloat16"), "oneb": ("sbuf", [128, 480], "bfloat16"), "e2": ("sbuf", [128, 480], "bfloat16"),
-    "onef": ("sbuf", [128, 128], "float32"), "idn": ("sbuf", [128, 128], "float32"), "sct": ("sbuf", [128, 128], "float32"),
-    "msk": ("sbuf", [128, 480], "float32"), "iot": ("sbuf", [128, 1024], "float32"),
-    "win0": ("sbuf", [128, 1024], "float32"), "win1": ("sbuf", [128, 1024], "float32"),
-    "c1": ("sbuf", [128, 5 * ST + 3], "float32"), "c2": ("sbuf", [128, 1024], "float32"), "row": ("sbuf", [128, 5 * ST + 3], "float32"),
-    "rmp": ("sbuf", [128, 512], "float32"), "ks": ("sbuf", [128, 480], "float32"), "mg": ("sbuf", [128, 480], "float32"),
-    "sp1": ("sbuf", [128, 264], "float32"), "sp2": ("sbuf", [128, 256], "float32"), "sps": ("sbuf", [128, 96], "float32"),
-    "src": ("sbuf", [128, 776], "float32"),
-    "pr1": ("sbuf", [128, 1024], "float32"), "pr2": ("sbuf", [128, 1024], "float32"), "prs": ("sbuf", [128, 384], "float32"),
-    "b1": ("sbuf", [128, 256], "float32"), "b2": ("sbuf", [128, 256], "float32"), "bs": ("sbuf", [128, 96], "float32"),
-    "cb0": ("sbuf", [128, 768], "float32"), "cb1": ("sbuf", [128, 768], "float32"), "cb2": ("sbuf", [128, 768], "float32"),
-    "ysb": ("sbuf", [128, 768], "float32"),
-    "sb0": ("sbuf", [128, 96], "float32"), "sb1": ("sbuf", [128, 96], "float32"), "sb2": ("sbuf", [128, 96], "float32"),
-    "sb3": ("sbuf", [128, 96], "float32"), "sb4": ("sbuf", [128, 96], "float32"), "sb5": ("sbuf", [128, 96], "float32"),
-    "ps_s0": ("psum", [128, 512], "float32"), "ps_s1": ("psum", [128, 512], "float32"), "ps_s2": ("psum", [128, 512], "float32"),
-    "ps_y0": ("psum", [128, 512], "float32"), "ps_y1": ("psum", [128, 512], "float32"), "ps_w1": ("psum", [128, 512], "float32"),
-    "ps_w2": ("psum", [128, 512], "float32"), "ps_c": ("psum", [128, 512], "float32"),
-}
+
+def buffers(dtype, **cols):
+    return {n: ("sbuf", [128, c], dtype) for n, c in cols.items()}
+
+
+SCRATCH = {n: ("psum", [128, 512], F32) for n in ("ps_s0", "ps_s1", "ps_s2", "ps_y0", "ps_y1", "ps_w1", "ps_w2", "ps_c")}
+SCRATCH.update(buffers(I32, seqi=48, upi=128, sndi=16, upt=128, upz=128))
+SCRATCH.update(buffers(U16, seq16=48, up16=128, sa16=12, ls=12, cmpz=6))
+SCRATCH.update(buffers(BF, qsb=768, rmb=768, cob=2048, scb=16, oneb=128, e2=128))
+SCRATCH.update(buffers(F32, onef=128, idn=128, sct=128, msk=128, iot=768, row=264, win0=1024, win1=1024, c1=1024, c2=1024,
+                       rmp=768, mgz=96, mgz2=48, mgz4=24, mgz8=12, mgz16=6, sp1=256, sp2=256, pr1=1032, pr2=1024, b1=264, b2=256,
+                       g3=96, cb0=776, cb1=776, cb2=776, ysb=768, sb0=96, sb1=96, sb2=96, sb3=96, sb4=96, sb5=96))
 LOADS = ["seqi", "upi", "sndi", "qsb", "rmb", "co1", "co2", "scb"]
 SEMAPHORES = (["q_v", "q_a", "q_p", "q_g", "sent", "y0", "y1"] + ["ld_" + n for n in LOADS] + ["arr%d" % i for i in range(6)])
 
@@ -108,7 +97,7 @@ def rank_program(g, core, T, topo):
 
     def ap(x):
         p = x[3] if len(x) > 3 else 128
-        return T[x[0]][0:p, x[1]:x[2]]
+        return T[x[0]][0:p, x[1]:x[2]] if len(x) < 5 else T[x[0]][0:p, x[1]:x[2]:x[4]]
 
     def ind(w, o):
         return T[w[0]][:, w[1]:w[2]].indirect(T[o[0]][:, o[1]:o[2]])
@@ -116,14 +105,14 @@ def rank_program(g, core, T, topo):
     def load(q, sem, dst, src_ap):
         emit(q, lambda: eng[q].dma_start(ap(dst), src_ap), [], [dst], sem="ld_" + sem, n=16)
 
-    def fill(x, v, ap_=None):
-        emit("v", lambda: g.vector.memset(ap_ if ap_ is not None else ap(x), v), [], [x])
+    def fill(x, v):
+        emit("v", lambda: g.vector.memset(ap(x), v), [], [x])
 
     def tt(out, a, b, op):
         emit("v", lambda: g.vector.tensor_tensor(ap(out), ap(a), ap(b), op), [a, b], [out])
 
-    def gtt(out, w, o, b):
-        emit("v", lambda: g.vector.tensor_tensor(ap(out), ind(w, o), ap(b), A.mult), [w, o, b], [out])
+    def gtt(out, w, o, b, op=A.mult):
+        emit("v", lambda: g.vector.tensor_tensor(ap(out), ind(w, o), ap(b), op), [w, o, b], [out])
 
     def gv(out, w, o):
         emit("v", lambda: g.vector.tensor_copy(ap(out), ind(w, o)), [w, o], [out])
@@ -143,13 +132,12 @@ def rank_program(g, core, T, topo):
         else:
             emit("v", lambda: g.vector.tensor_scalar(ap(out), ap(a), s1, s2, op0, op1), [a], [out])
 
-    def mm(out, l, r, start, stop, rhs=None):
-        emit("p", lambda: g.tensor.matmul(ap(out), ap(l), rhs if rhs is not None else ap(r), start, stop), [l, r], [out])
+    def mm(out, l, r, start, stop):
+        emit("p", lambda: g.tensor.matmul(ap(out), ap(l), ap(r), start, stop), [l, r], [out])
 
     IDN = ("idn", 0, 128)
 
-    def scatter_copy(cb, w, a):
-        o = ("seq16", 16 * w, 16 * w + 16)
+    def scatter_copy(cb, o, a):
         emit("v", lambda: g.vector.tensor_copy(ind((cb, 0, 768), o), ap(a)), [o, a], [(cb, 0, 768)])
 
     myplan = plan(core, cores, topo)
@@ -175,8 +163,8 @@ def rank_program(g, core, T, topo):
             note("net", [], [("win%d" % (k % 2), a, a + 32)], ("arr%d" % i, tot))
 
     load("s", "seqi", ("seqi", 0, 48), T.seq[:, :])
-    load("a", "qsb", ("qsb", 0, 768), T.qs[:, :])
-    load("s", "rmb", ("rmb", 0, 768), T.rm[:, :])
+    load("a", "rmb", ("rmb", 0, 768), T.rm[:, :])
+    load("s", "qsb", ("qsb", 0, 768), T.qs[:, :])
     load("a", "sndi", ("sndi", 0, 16), T.snd[:, :])
     load("s", "upi", ("upi", 0, 128), T.up[:, 64:192])
     load("s", "co1", ("cob", 0, 1024), T.co[:, 1024:2048])
@@ -184,23 +172,23 @@ def rank_program(g, core, T, topo):
     load("s", "scb", ("scb", 0, 16, 16), T.sc[:, :])
 
     fill(("onef", 0, 128), 1.0)
-    fill(("oneb", 0, 480, 16), 1.0)
+    fill(("oneb", 0, 128, 16), 1.0)
     emit("g", lambda: g.affine_select(T.idn[:, :], T.onef[:, :], [[-1, 128]], A.is_equal, 0.0, 0, 1), [("onef", 0, 128)], [IDN])
-    emit("g", lambda: g.affine_select(T.e2[0:16, :], T.oneb[0:16, :], [[0, 30], [1, 16]], A.is_equal, 0.0, 0, -1),
-         [("oneb", 0, 480)], [("e2", 0, 480)])
+    emit("g", lambda: g.affine_select(T.e2[0:16, :], T.oneb[0:16, :], [[0, 8], [1, 16]], A.is_equal, 0.0, 0, -1),
+         [("oneb", 0, 128)], [("e2", 0, 128)])
     for b in ("win0", "win1"):
         fill((b, 256, SL), 0.0)
         for w in (0, 1):
             lo = SL + (w * len(cores) + rank) * 32
             fill((b, lo, lo + 32), 0.0)
-    fill(("c1", 0, 5 * ST), 0.0, T.c1[:, 256:5 * ST:ST])
-    fill(("row", 0, 4 * ST), float(ZC), T.row[:, 256:4 * ST:ST])
-    fill(("row", 5 * ST - 1, 5 * ST), 768.0)
-    fill(("sp1", 256, 264), 0.0)
-    fill(("src", 768, 776), 0.0)
+    fill(("row", 256, 264), 768.0)
+    fill(("b1", 256, 264), 0.0)
+    fill(("pr1", 1024, 1032), 0.0)
+    fill(("cb1", 768, 776), 0.0)
+    fill(("cb2", 768, 776), 0.0)
 
-    RM0 = ("c1", 4 * ST, 4 * ST + 256)
     SEQ = [("seq16", 16 * w, 16 * w + 16) for w in range(3)]
+    RMP = [("rmp", 256 * w, 256 * w + 256) for w in range(3)]
     cpv(("seq16", 0, 48), ("seqi", 0, 48))
 
     def snd_list(w):
@@ -213,109 +201,104 @@ def rank_program(g, core, T, topo):
             ts(("sa16", 6 * w + 2 * j, 6 * w + 2 * (j + n)), ("sndi", a, a + 2 * n), float(ZC), None, A.min)
             j += n
 
+    ga(RMP[0], ("rmb", 0, 768), SEQ[0])
     snd_list(0)
-    ga(RM0, ("rmb", 0, 768), SEQ[0])
-    gtt(("win0", 0, 256), ("qsb", 0, 768), SEQ[0], RM0)
+    gtt(("win0", 0, 256), ("qsb", 0, 768), SEQ[0], RMP[0])
     gv(("sb0", 0, 96), ("win0", 0, 520), ("sa16", 0, 6))
     send(0, 0)
-    emit("g", lambda: g.iota(T.iot[:, :], [[1, 1024]], 0, 0, allow_small_or_imprecise_dtypes=True), [], [("iot", 0, 1024)])
+    emit("g", lambda: g.iota(T.iot[:, :], [[1, 768]], 0, 0, allow_small_or_imprecise_dtypes=True), [], [("iot", 0, 768)])
 
-    RMP = [("rmp", 0, 256), ("rmp", 256, 512)]
-    PRM = [("ps_c", 0, 256), ("ps_s2", 0, 256)]
-    for w in (0, 1):
-        ga(RMP[w], ("rmb", 0, 768), SEQ[w + 1])
+    PRM = [None, ("ps_c", 0, 256), ("ps_s2", 0, 256)]
+    for w in (1, 2):
+        ga(RMP[w], ("rmb", 0, 768), SEQ[w])
         cpa(PRM[w], RMP[w])
-    mm(("ps_s0", 0, 480), ("e2", 0, 128, 16), ("e2", 0, 480, 16), True, True)
-    for o in range(8):
-        mm(("ps_s1", 16 * o, 16 * o + 16), ("e2", 0, 128, 16), ("scb", 0, 16, 16), True, True)
+    mm(("ps_s0", 0, 128), ("e2", 0, 128, 16), ("e2", 0, 128, 16), True, True)
     ts(("upt", 0, 128), ("upi", 0, 128), 1024.0, float(ZC - 1024), A.is_equal, A.mult)
     tt(("upz", 0, 128), ("upi", 0, 128), ("upt", 0, 128), A.add)
     cpv(("up16", 0, 128), ("upz", 0, 128))
-    gtt(("sp1", 0, 256), ("qsb", 0, 768), SEQ[1], RMP[0])
+    gtt(("sp1", 0, 256), ("qsb", 0, 768), SEQ[1], RMP[1])
     mm(("ps_w1", 0, 256), IDN, ("sp1", 0, 256), True, False)
     for u in range(4):
-        tt(("c1", ST * u, ST * u + 256), ("cob", 256 * u, 256 * u + 256), PRM[0], A.mult)
-    gtt(("sp2", 0, 256), ("qsb", 0, 768), SEQ[2], RMP[1])
-    mm(("ps_w2", 0, 256), IDN, ("sp2", 0, 256), True, False)
-    for u in range(4):
-        tt(("c2", 256 * u, 256 * u + 256), ("cob", 1024 + 256 * u, 1280 + 256 * u), PRM[1], A.mult)
+        tt(("c1", 256 * u, 256 * u + 256), ("cob", 256 * u, 256 * u + 256), PRM[1], A.mult)
     snd_list(1)
-    cpa(("msk", 0, 480), ("ps_s0", 0, 480))
+    LS1, LS0 = ("ls", 0, 6), ("ls", 6, 12)
+    ts(LS1, ("sa16", 6, 12), -256.0, None, A.add)
+    gtt(("sp2", 0, 256), ("qsb", 0, 768), SEQ[2], RMP[2])
+    mm(("ps_w2", 0, 256), IDN, ("sp2", 0, 256), True, False)
+    for o in range(8):
+        mm(("ps_s1", 16 * o, 16 * o + 16), ("e2", 0, 128, 16), ("scb", 0, 16, 16), True, True)
+    cpa(("msk", 0, 128), ("ps_s0", 0, 128))
+    ga(("row", 0, 256), ("iot", 0, 768), SEQ[0])
     cpa(("sct", 0, 128), ("ps_s1", 0, 128))
-    for u in range(4):
-        ga(("row", ST * u, ST * u + 256), ("iot", 0, 1024), ("up16", 16 * u, 16 * u + 16))
-    ga(("row", ST * 4, ST * 4 + 256), ("iot", 0, 1024), SEQ[0])
 
-    def psi1(b):
-        for u in range(4):
-            gtt(("pr1", 256 * u, 256 * u + 256), (b, 0, 896), ("up16", 16 * u, 16 * u + 16), ("c1", ST * u, ST * u + 256))
+    def coef2(u):
+        tt(("c2", 256 * u, 256 * u + 256), ("cob", 1024 + 256 * u, 1280 + 256 * u), PRM[2], A.mult)
+
+    coef2(0)
+    coef2(1)
+
+    def products(w, b, end):
+        pr, c, ps = "pr%d" % w, "c%d" % w, "ps_w%d" % w
+        for u, n in ((0, 1), (1, 1), (2, 2)):
+            x = (256 * u, 256 * (u + n))
+            gtt((pr,) + x, (b, 0, end), ("up16", 64 * w - 64 + 16 * u, 64 * w - 64 + 16 * (u + n)), (c,) + x)
             if u < 2:
-                mm(("ps_w1", 0, 256), IDN, ("pr1", 256 * u, 256 * u + 256), False, u == 1)
-        tt(("b1", 0, 256), ("pr1", 512, 768), ("ps_w1", 0, 256), A.add)
+                mm((ps, 0, 256), IDN, (pr,) + x, False, u == 1)
+        if w == 1:
+            ga(("g3", 0, 96), (pr, 768, 1025), LS1)
+        tt(("b%d" % w, 0, 256), (pr, 512, 768), (ps, 0, 256), A.add)
+
+    def wave1(k, b):
+        products(1, b, 896)
+        gtt(("sb%d" % (2 * k + 1), 0, 96), ("b1", 0, 257), LS1, ("g3", 0, 96), A.add)
+        send(k, 1)
         tt((b, 256, 512), ("b1", 0, 256), ("pr1", 768, 1024), A.add)
 
-    def psi2(b, cb):
-        for u, n in ((0, 1), (1, 1), (2, 2)):
-            c = (256 * u, 256 * (u + n))
-            gtt(("pr2",) + c, (b, 0, 1024), ("up16", 64 + 16 * u, 64 + 16 * (u + n)), ("c2",) + c)
-            if u < 2:
-                mm(("ps_w2", 0, 256), IDN, ("pr2",) + c, False, u == 1)
-        tt(("b2", 0, 256), ("pr2", 512, 768), ("ps_w2", 0, 256), A.add)
+    def wave2(b, cb):
+        products(2, b, 1024)
         x, y, o = ("b2", 0, 256), ("pr2", 768, 1024), SEQ[2]
         emit("v", lambda: g.vector.tensor_tensor(ind((cb, 0, 768), o), ap(x), ap(y), A.add), [x, y, o], [(cb, 0, 768)])
 
     def flux(k):
-        for h in (0, 1):
-            mm(("ps_y%d" % h, 0, 384, 16), ("msk", 0, 16), ("cb%d" % k, 384 * h, 384 * h + 384), k == 0, k == SW - 1)
+        for h, (lo, hi) in enumerate(YC):
+            mm(("ps_y%d" % h, 0, hi - lo, 16), ("msk", 0, 16), ("cb%d" % k, lo, hi), k == 0, k == SW - 1)
 
-    psi1("win0")
-    gv(("sb1", 0, 96), ("win0", 0, 520), ("sa16", 6, 12))
-    send(0, 1)
-    scatter_copy("cb0", 0, ("win0", 0, 256))
-    for u in range(4):
-        ts(("lst2", 6 * u, 6 * u + 6), ("sa16", 6, 12), float(ST * u - 256), None, A.add)
-    ts(("lst2", 24, 30), ("sa16", 0, 6), 256.0, float(4 * ST), A.min, A.add)
-    gtt(("mg", 0, 480), ("row", 0, 5 * ST), ("lst2", 0, 30), ("msk", 0, 480))
-    for j in range(16):
-        mm(("ps_s1", 0, 30), IDN, ("mg", 0, 480), j == 0, j == 15, rhs=T.mg[:, j:480:16])
-    ga(("ks", 0, 480), ("c1", 0, 5 * ST), ("lst2", 0, 30))
-    scatter_copy("cb0", 1, ("win0", 256, 512))
-    cpv(("cmp16", 0, 30), ("ps_s1", 0, 30))
-    psi2("win0", "cb0")
+    wave1(0, "win0")
+    coef2(2)
+    coef2(3)
+    scatter_copy("cb0", ("seq16", 0, 32), ("win0", 0, 512))
+    wave2("win0", "cb0")
 
     for k in range(1, SW):
         b, cb = "win%d" % (k % 2), "cb%d" % k
         for i, (lo, hi) in enumerate(CH):
             p = ("ps_s%d" % i, 0, hi - lo)
             mm(p, ("sct", 0, 128), ("cb%d" % (k - 1), lo, hi), True, True)
-            (cpa if i == 1 else cpv)(("src", lo, hi), p)
-        gtt(("sb%d" % (2 * k), 0, 96), ("src", 0, 769), ("cmp16", 24, 30), ("ks", 384, 480))
+            if i == 0 and k == 1:
+                ts(LS0, ("sa16", 0, 6), 256.0, None, A.min)
+                gtt(("mgz", 0, 96), ("row", 0, 257), LS0, ("msk", 0, 96))
+                for m in (1, 2, 4, 8):
+                    x = "mgz" + (str(m) if m > 1 else "")
+                    tt(("mgz%d" % (2 * m), 0, 48 // m), (x, 0, 96 // m, 128, 2), (x, 1, 96 // m, 128, 2), A.add)
+                cpv(("cmpz", 0, 6), ("mgz16", 0, 6))
+            tt((cb, lo, hi), p, ("rmb", lo, hi), A.mult)
+        gv(("sb%d" % (2 * k), 0, 96), (cb, 0, 769), ("cmpz", 0, 6))
         send(k, 0)
-        gtt(("sp1", 0, 256), ("src", 0, 769), SEQ[1], RMP[0])
-        gv(("sps", 0, 96), ("sp1", 0, 257), ("lst2", 0, 6))
-        mm(("ps_c", 0, 96), IDN, ("sps", 0, 96), True, False)
-        gtt((b, 0, 256), ("src", 0, 769), SEQ[0], RM0)
-        mm(("ps_w1", 0, 256), IDN, ("sp1", 0, 256), True, False)
-        gtt(("sp2", 0, 256), ("src", 0, 769), SEQ[2], RMP[1])
-        mm(("ps_w2", 0, 256), IDN, ("sp2", 0, 256), True, False)
-        scatter_copy(cb, 0, (b, 0, 256))
-        for u, n in ((0, 1), (1, 1), (2, 2)):
-            c = (96 * u, 96 * (u + n))
-            gtt(("prs",) + c, (b, 0, 896), ("cmp16", 6 * u, 6 * (u + n)), ("ks",) + c)
-            if u < 2:
-                mm(("ps_c", 0, 96), IDN, ("prs",) + c, False, u == 1)
-        tt(("bs", 0, 96), ("prs", 192, 288), ("ps_c", 0, 96), A.add)
-        tt(("sb%d" % (2 * k + 1), 0, 96), ("bs", 0, 96), ("prs", 288, 384), A.add)
-        send(k, 1)
-        psi1(b)
-        scatter_copy(cb, 1, (b, 256, 512))
+        gv((b, 0, 256), (cb, 0, 768), SEQ[0])
+        for w in (1, 2):
+            sp = ("sp%d" % w, 0, 256)
+            ga(sp, (cb, 0, 768), SEQ[w])
+            mm(("ps_w%d" % w, 0, 256), IDN, sp, True, False)
+        wave1(k, b)
         flux(k - 1)
-        psi2(b, cb)
+        scatter_copy(cb, SEQ[1], (b, 256, 512))
+        wave2(b, cb)
     flux(SW - 1)
 
     for h, cp, q in ((0, cpv, "s"), (1, cpa, "a")):
-        x = ("ysb", 384 * h, 384 * h + 384, 16)
-        cp(x, ("ps_y%d" % h, 0, 384, 16))
-        emit(q, lambda: eng[q].dma_start(T.y[:, 384 * h:384 * h + 384], ap(x)), [x], [], sem="y%d" % h, n=16)
+        lo, hi = YC[h]
+        x = ("ysb", lo, hi, 16)
+        cp(x, ("ps_y%d" % h, 0, hi - lo, 16))
+        emit(q, lambda: eng[q].dma_start(T.y[:, lo:hi], ap(x)), [x], [], sem="y%d" % h, n=16)
     for s in ("q_v", "q_a", "q_p", "q_g", "y0", "y1", "sent"):
         g.wait_ge(T.sem[s], count[s])

@@ -4,8 +4,9 @@ from concourse.mybir import AluOpType, ActivationFunctionType
 SW = 3
 ZC = 512
 SL = 768
-CH = [(0, 320), (320, 592), (592, 768)]
-YC = [(0, 512), (512, 768)]
+CH = [(0, 416), (416, 656), (656, 768)]
+YC = [(0, 448), (448, 768)]
+CUT = [(0, 96), (96, 256), (256, 512)]
 F32, BF, I32, U16 = "float32", "bfloat16", "int32", "uint16"
 
 
@@ -13,13 +14,14 @@ def buffers(dtype, **cols):
     return {n: ("sbuf", [128, c], dtype) for n, c in cols.items()}
 
 
-SCRATCH = {n: ("psum", [128, 512], F32) for n in ("ps_s0", "ps_s1", "ps_s2", "ps_y0", "ps_y1", "ps_w1", "ps_w2", "ps_c")}
-SCRATCH.update(buffers(I32, seqi=48, upi=128, sndi=16, upt=128, upz=128))
-SCRATCH.update(buffers(U16, seq16=48, up16=128, sa16=12, ls=12, cmpz=6))
+SCRATCH = {n: ("psum", [128, 512], F32) for n in ("ps_s0", "ps_s1", "ps_s2", "ps_y0", "ps_y1", "ps_w", "ps_c1", "ps_c2")}
+SCRATCH.update(buffers(I32, seqi=48, upi=128, sndi=16, upt=64, upz=64))
+SCRATCH.update(buffers(U16, seq16=48, up16=128, ls=12, cmpz=6))
 SCRATCH.update(buffers(BF, qsb=768, rmb=768, cob=2048, scb=16, oneb=128, e2=128))
-SCRATCH.update(buffers(F32, onef=128, idn=128, sct=128, msk=128, iot=768, row=264, win0=1024, win1=1024, c1=1024, c2=1024,
-                       rmp=768, mgz=96, mgz2=48, mgz4=24, mgz8=12, mgz16=6, sp1=256, sp2=256, pr1=1032, pr2=1024, b1=264, b2=256,
-                       g3=96, cb0=776, cb1=776, cb2=776, ysb=768, sb0=96, sb1=96, sb2=96, sb3=96, sb4=96, sb5=96))
+SCRATCH.update(buffers(F32, onef=128, idn=128, sct=128, msk=128, iot=768, row=264, win0=1032, win1=1032, c1=512, c2=512,
+                       qp=264, rp=264, rps=96, rmp=512, mgz=96, keep=96, run=96, sp1=256, sp2=256, pr1=1032, pr2=1024,
+                       b1=264, b2=256, h1=512, h2=512, g3=96, cb0=776, cb1=776, cb2=776, ysb=768,
+                       sb0=96, sb1=96, sb2=96, sb3=96, sb4=96, sb5=96))
 LOADS = ["seqi", "upi", "sndi", "qsb", "rmb", "co1", "co2", "scb"]
 SEMAPHORES = (["q_v", "q_a", "q_p", "q_g", "sent", "y0", "y1"] + ["ld_" + n for n in LOADS] + ["arr%d" % i for i in range(6)])
 
@@ -28,13 +30,7 @@ def plan(src, cores, topo):
     dst = [c for c in cores if c != src]
     far = [c for c in dst if topo.die(c) != topo.die(src)]
     near = [c for c in dst if topo.die(c) == topo.die(src)]
-    res = {}
-    for group, first in ((far, 0), (near, 1)):
-        for i, d in enumerate(group):
-            e = topo.engines(src, d)[first::2]
-            n = len(e) // len(group)
-            res[d] = e[i * n:(i + 1) * n]
-    return res
+    return [[(d, topo.engines(src, d)[i::len(grp)]) for i, d in enumerate(grp)] for grp in (far, near) if grp]
 
 
 def rank_program(g, core, T, topo):
@@ -68,7 +64,7 @@ def rank_program(g, core, T, topo):
                 psum = n[:3] == "ps_"
                 for (l2, h2, kind, tok, q2) in hist.get(n, []):
                     if psum:
-                        hit = q2 != q
+                        hit = q2 != q or (q != "p" and l2 < hi and lo < h2 and (kind == "w" or not w))
                     else:
                         hit = l2 < hi and lo < h2 and (kind == "w" or not w)
                     if hit and toks.get(tok[0], 0) < tok[1]:
@@ -137,27 +133,28 @@ def rank_program(g, core, T, topo):
 
     IDN = ("idn", 0, 128)
 
-    def scatter_copy(cb, o, a):
-        emit("v", lambda: g.vector.tensor_copy(ind((cb, 0, 768), o), ap(a)), [o, a], [(cb, 0, 768)])
-
-    myplan = plan(core, cores, topo)
+    def scatter_sum(w, cb):
+        x, y, o = ("b%d" % w, 0, 256), ("pr%d" % w, 768, 1024), ("seq16", 16 * w, 16 * w + 16)
+        emit("v", lambda: g.vector.tensor_tensor(ind((cb, 0, 768), o), ap(x), ap(y), A.add), [x, y, o], [(cb, 0, 768)])
 
     def send(k, w):
         i = 2 * k + w
         sb = "sb%d" % i
         deps("g", [(sb, 0, 96)], [])
-        tr = []
         lo = SL + (w * len(cores) + rank) * 32
-        for j, d in enumerate(others):
-            rid, pid = topo.addr(cores[d])[:2]
-            m = 0
-            for e in myplan[cores[d]]:
-                m |= 1 << e
-            tr.append(RemoteDMATransfer(dst_ids=[DstId(rid=rid, pnc=pid)], dma_engine_mask=m, remote_sem=T.sem["arr%d" % i],
-                                        src=T[sb][:, 32 * j:32 * j + 32], dst=T["win%d" % (k % 2)][:, lo:lo + 32]))
-            count["sent"] = count.get("sent", 0) + len(myplan[cores[d]])
-        g.remote_dma_fused(tr, local_sem=T.sem.sent)
-        tot = sum(len(plan(cores[d], cores, topo)[core]) for d in others)
+        for call in plan(core, cores, topo):
+            tr = []
+            for c, engines in call:
+                j = others.index(cores.index(c))
+                rid, pid = topo.addr(c)[:2]
+                m = 0
+                for e in engines:
+                    m |= 1 << e
+                tr.append(RemoteDMATransfer(dst_ids=[DstId(rid=rid, pnc=pid)], dma_engine_mask=m, remote_sem=T.sem["arr%d" % i],
+                                            src=T[sb][:, 32 * j:32 * j + 32], dst=T["win%d" % (k % 2)][:, lo:lo + 32]))
+                count["sent"] = count.get("sent", 0) + len(engines)
+            g.remote_dma_fused(tr, local_sem=T.sem.sent)
+        tot = sum(len(e) for d in others for call in plan(cores[d], cores, topo) for c, e in call if c == core)
         for d in others:
             a = SL + (w * len(cores) + d) * 32
             note("net", [], [("win%d" % (k % 2), a, a + 32)], ("arr%d" % i, tot))
@@ -176,8 +173,11 @@ def rank_program(g, core, T, topo):
     emit("g", lambda: g.affine_select(T.idn[:, :], T.onef[:, :], [[-1, 128]], A.is_equal, 0.0, 0, 1), [("onef", 0, 128)], [IDN])
     emit("g", lambda: g.affine_select(T.e2[0:16, :], T.oneb[0:16, :], [[0, 8], [1, 16]], A.is_equal, 0.0, 0, -1),
          [("oneb", 0, 128)], [("e2", 0, 128)])
+    fill(("qp", 256, 264), 0.0)
+    fill(("rp", 256, 264), 0.0)
     for b in ("win0", "win1"):
         fill((b, 256, SL), 0.0)
+        fill((b, 1024, 1032), 0.0)
         for w in (0, 1):
             lo = SL + (w * len(cores) + rank) * 32
             fill((b, lo, lo + 32), 0.0)
@@ -186,9 +186,11 @@ def rank_program(g, core, T, topo):
     fill(("pr1", 1024, 1032), 0.0)
     fill(("cb1", 768, 776), 0.0)
     fill(("cb2", 768, 776), 0.0)
+    fill(("keep", 0, 96), 1.0)
+    fill(("keep", 0, 96, 128, 16), 0.0)
 
     SEQ = [("seq16", 16 * w, 16 * w + 16) for w in range(3)]
-    RMP = [("rmp", 256 * w, 256 * w + 256) for w in range(3)]
+    LS = [("ls", 0, 6), ("ls", 6, 12)]
     cpv(("seq16", 0, 48), ("seqi", 0, 48))
 
     def snd_list(w):
@@ -198,76 +200,97 @@ def rank_program(g, core, T, topo):
             while j + n < 3 and others[j + n] == others[j] + n:
                 n += 1
             a = 8 * w + 2 * others[j]
-            ts(("sa16", 6 * w + 2 * j, 6 * w + 2 * (j + n)), ("sndi", a, a + 2 * n), float(ZC), None, A.min)
+            o, x = ("ls", 6 * w + 2 * j, 6 * w + 2 * (j + n)), ("sndi", a, a + 2 * n)
+            if w:
+                ts(o, x, 512.0, -256.0, A.min, A.add)
+            else:
+                ts(o, x, 256.0, None, A.min)
             j += n
 
-    ga(RMP[0], ("rmb", 0, 768), SEQ[0])
+    ga(("rp", 0, 256), ("rmb", 0, 768), SEQ[0])
     snd_list(0)
-    gtt(("win0", 0, 256), ("qsb", 0, 768), SEQ[0], RMP[0])
-    gv(("sb0", 0, 96), ("win0", 0, 520), ("sa16", 0, 6))
+    ga(("rps", 0, 96), ("rp", 0, 257), LS[0])
+    gv(("qp", 0, 256), ("qsb", 0, 768), SEQ[0])
+    gtt(("sb0", 0, 96), ("qp", 0, 257), LS[0], ("rps", 0, 96))
     send(0, 0)
     emit("g", lambda: g.iota(T.iot[:, :], [[1, 768]], 0, 0, allow_small_or_imprecise_dtypes=True), [], [("iot", 0, 768)])
 
-    PRM = [None, ("ps_c", 0, 256), ("ps_s2", 0, 256)]
+    RMP = [None, ("rmp", 0, 256), ("rmp", 256, 512)]
+    PRM = [None, ("ps_s1", 0, 256), ("ps_s2", 0, 256)]
+    RMC = [(("ps_y0", 0, 512), 0, 512), (("ps_y1", 0, 256), 512, 768)]
+    for p, lo, hi in RMC:
+        cpa(p, ("rmb", lo, hi))
     for w in (1, 2):
         ga(RMP[w], ("rmb", 0, 768), SEQ[w])
         cpa(PRM[w], RMP[w])
+    ts(("upt", 0, 64), ("upi", 0, 64), 1024.0, float(ZC - 1024), A.is_equal, A.mult)
+    tt(("upz", 0, 64), ("upi", 0, 64), ("upt", 0, 64), A.add)
+    cpv(("up16", 0, 64), ("upz", 0, 64))
+    for p, lo, hi in RMC:
+        tt(("cb0", lo, hi), ("qsb", lo, hi), p, A.mult)
+    ga(("win0", 0, 256), ("cb0", 0, 768), SEQ[0])
+    for w in (1, 2):
+        ga(("sp%d" % w, 0, 256), ("cb0", 0, 768), SEQ[w])
+
+    def coef(w, us):
+        for u in us:
+            out = ("c%d" % w, 256 * u, 256 * u + 256) if u < 2 else ("ps_c%d" % w, 256 * u - 512, 256 * u - 256)
+            c = 1024 * (w - 1) + 256 * u
+            tt(out, ("cob", c, c + 256), PRM[w], A.mult)
+
+    def presum(w):
+        mm(("ps_w", 0, 256), IDN, ("sp%d" % w, 0, 256), True, False)
+
     mm(("ps_s0", 0, 128), ("e2", 0, 128, 16), ("e2", 0, 128, 16), True, True)
-    ts(("upt", 0, 128), ("upi", 0, 128), 1024.0, float(ZC - 1024), A.is_equal, A.mult)
-    tt(("upz", 0, 128), ("upi", 0, 128), ("upt", 0, 128), A.add)
-    cpv(("up16", 0, 128), ("upz", 0, 128))
-    gtt(("sp1", 0, 256), ("qsb", 0, 768), SEQ[1], RMP[1])
-    mm(("ps_w1", 0, 256), IDN, ("sp1", 0, 256), True, False)
-    for u in range(4):
-        tt(("c1", 256 * u, 256 * u + 256), ("cob", 256 * u, 256 * u + 256), PRM[1], A.mult)
+    presum(1)
+    coef(1, (0, 1, 2, 3))
     snd_list(1)
-    LS1, LS0 = ("ls", 0, 6), ("ls", 6, 12)
-    ts(LS1, ("sa16", 6, 12), -256.0, None, A.add)
-    gtt(("sp2", 0, 256), ("qsb", 0, 768), SEQ[2], RMP[2])
-    mm(("ps_w2", 0, 256), IDN, ("sp2", 0, 256), True, False)
-    for o in range(8):
-        mm(("ps_s1", 16 * o, 16 * o + 16), ("e2", 0, 128, 16), ("scb", 0, 16, 16), True, True)
-    cpa(("msk", 0, 128), ("ps_s0", 0, 128))
-    ga(("row", 0, 256), ("iot", 0, 768), SEQ[0])
-    cpa(("sct", 0, 128), ("ps_s1", 0, 128))
+    coef(2, (0, 1, 2))
+    cpv(("up16", 64, 128), ("upi", 64, 128))
 
-    def coef2(u):
-        tt(("c2", 256 * u, 256 * u + 256), ("cob", 1024 + 256 * u, 1280 + 256 * u), PRM[2], A.mult)
+    def flux(k, h):
+        lo, hi = YC[h]
+        mm(("ps_y%d" % h, 0, hi - lo, 16), ("msk", 0, 16), ("cb%d" % k, lo, hi), k == 0, k == SW - 1)
 
-    coef2(0)
-    coef2(1)
+    def spare(k):
+        if k > 0:
+            flux(k - 1, 1)
+            return
+        for o in range(8):
+            mm(("ps_s0", 128 + 16 * o, 144 + 16 * o), ("e2", 0, 128, 16), ("scb", 0, 16, 16), True, True)
+        ga(("row", 0, 256), ("iot", 0, 768), SEQ[0])
+        cpa(("msk", 0, 128), ("ps_s0", 0, 128))
+        cpa(("sct", 0, 128), ("ps_s0", 128, 256))
 
-    def products(w, b, end):
-        pr, c, ps = "pr%d" % w, "c%d" % w, "ps_w%d" % w
-        for u, n in ((0, 1), (1, 1), (2, 2)):
-            x = (256 * u, 256 * (u + n))
-            gtt((pr,) + x, (b, 0, end), ("up16", 64 * w - 64 + 16 * u, 64 * w - 64 + 16 * (u + n)), (c,) + x)
-            if u < 2:
-                mm((ps, 0, 256), IDN, (pr,) + x, False, u == 1)
+    def products(w, b, end, k):
+        pr, h, ps = "pr%d" % w, ("h%d" % w, 0, 512), ("ps_w", 0, 256)
+        up = 64 * (w - 1)
+        ga(h, (b, 0, end), ("up16", up + 32, up + 64))
+        for lo, hi in CUT:
+            gtt((pr, lo, hi), (b, 0, end), ("up16", up + lo // 16, up + hi // 16), ("c%d" % w, lo, hi))
+            mm(("ps_w", lo % 256, (hi - 1) % 256 + 1), IDN, (pr, lo, hi), False, hi == 512)
+        tt((pr, 512, 1024), h, ("ps_c%d" % w, 0, 512), A.mult)
         if w == 1:
-            ga(("g3", 0, 96), (pr, 768, 1025), LS1)
-        tt(("b%d" % w, 0, 256), (pr, 512, 768), (ps, 0, 256), A.add)
+            ga(("g3", 0, 96), (pr, 768, 1025), LS[1])
+        else:
+            spare(k)
+        tt(("b%d" % w, 0, 256), (pr, 512, 768), ps, A.add)
 
     def wave1(k, b):
-        products(1, b, 896)
-        gtt(("sb%d" % (2 * k + 1), 0, 96), ("b1", 0, 257), LS1, ("g3", 0, 96), A.add)
+        products(1, b, 896, k)
+        gtt(("sb%d" % (2 * k + 1), 0, 96), ("b1", 0, 257), LS[1], ("g3", 0, 96), A.add)
         send(k, 1)
         tt((b, 256, 512), ("b1", 0, 256), ("pr1", 768, 1024), A.add)
+        presum(2)
 
-    def wave2(b, cb):
-        products(2, b, 1024)
-        x, y, o = ("b2", 0, 256), ("pr2", 768, 1024), SEQ[2]
-        emit("v", lambda: g.vector.tensor_tensor(ind((cb, 0, 768), o), ap(x), ap(y), A.add), [x, y, o], [(cb, 0, 768)])
-
-    def flux(k):
-        for h, (lo, hi) in enumerate(YC):
-            mm(("ps_y%d" % h, 0, hi - lo, 16), ("msk", 0, 16), ("cb%d" % k, lo, hi), k == 0, k == SW - 1)
+    def wave2(k, b, cb):
+        products(2, b, 1025, k)
+        scatter_sum(2, cb)
 
     wave1(0, "win0")
-    coef2(2)
-    coef2(3)
-    scatter_copy("cb0", ("seq16", 0, 32), ("win0", 0, 512))
-    wave2("win0", "cb0")
+    scatter_sum(1, "cb0")
+    coef(2, (3,))
+    wave2(0, "win0", "cb0")
 
     for k in range(1, SW):
         b, cb = "win%d" % (k % 2), "cb%d" % k
@@ -275,27 +298,24 @@ def rank_program(g, core, T, topo):
             p = ("ps_s%d" % i, 0, hi - lo)
             mm(p, ("sct", 0, 128), ("cb%d" % (k - 1), lo, hi), True, True)
             if i == 0 and k == 1:
-                ts(LS0, ("sa16", 0, 6), 256.0, None, A.min)
-                gtt(("mgz", 0, 96), ("row", 0, 257), LS0, ("msk", 0, 96))
-                for m in (1, 2, 4, 8):
-                    x = "mgz" + (str(m) if m > 1 else "")
-                    tt(("mgz%d" % (2 * m), 0, 48 // m), (x, 0, 96 // m, 128, 2), (x, 1, 96 // m, 128, 2), A.add)
-                cpv(("cmpz", 0, 6), ("mgz16", 0, 6))
+                gtt(("mgz", 0, 96), ("row", 0, 257), LS[0], ("msk", 0, 96))
+                r, m, x = ("run", 0, 96), ("keep", 0, 96), ("mgz", 0, 96)
+                emit("v", lambda: g.vector.tensor_tensor_scan(ap(r), ap(m), ap(x), 0.0, A.mult, A.add), [m, x], [r])
+                cpv(("cmpz", 0, 6), ("run", 15, 96, 128, 16))
             tt((cb, lo, hi), p, ("rmb", lo, hi), A.mult)
         gv(("sb%d" % (2 * k), 0, 96), (cb, 0, 769), ("cmpz", 0, 6))
         send(k, 0)
         gv((b, 0, 256), (cb, 0, 768), SEQ[0])
         for w in (1, 2):
-            sp = ("sp%d" % w, 0, 256)
-            ga(sp, (cb, 0, 768), SEQ[w])
-            mm(("ps_w%d" % w, 0, 256), IDN, sp, True, False)
+            ga(("sp%d" % w, 0, 256), (cb, 0, 768), SEQ[w])
+        presum(1)
         wave1(k, b)
-        flux(k - 1)
-        scatter_copy(cb, SEQ[1], (b, 256, 512))
-        wave2(b, cb)
-    flux(SW - 1)
+        flux(k - 1, 0)
+        scatter_sum(1, cb)
+        wave2(k, b, cb)
 
     for h, cp, q in ((0, cpv, "s"), (1, cpa, "a")):
+        flux(SW - 1, h)
         lo, hi = YC[h]
         x = ("ysb", lo, hi, 16)
         cp(x, ("ps_y%d" % h, 0, hi - lo, 16))

@@ -4,9 +4,10 @@ from concourse.mybir import AluOpType, ActivationFunctionType
 SW = 3
 ZC = 512
 SL = 768
-CH = [(0, 416), (416, 656), (656, 768)]
-YC = [(0, 448), (448, 768)]
-CUT = [(0, 96), (96, 256), (256, 512)]
+CUT = [(0, 96), (96, 256), (256, 448)]
+XA, XB = 448, 640
+CH = [("ps_s0", 0, 0, 416), ("ps_s1", 0, 416, 656), ("ps_w", 256, 656, 768)]
+NJ = 6
 F32, BF, I32, U16 = "float32", "bfloat16", "int32", "uint16"
 
 
@@ -14,13 +15,13 @@ def buffers(dtype, **cols):
     return {n: ("sbuf", [128, c], dtype) for n, c in cols.items()}
 
 
-SCRATCH = {n: ("psum", [128, 512], F32) for n in ("ps_s0", "ps_s1", "ps_s2", "ps_y0", "ps_y1", "ps_w", "ps_c1", "ps_c2")}
+SCRATCH = {n: ("psum", [128, 512], F32) for n in ("ps_s0", "ps_s1", "ps_y0", "ps_y1", "ps_w", "ps_c1", "ps_c2", "ps_c3")}
 SCRATCH.update(buffers(I32, seqi=48, upi=128, sndi=16, upt=64, upz=64))
 SCRATCH.update(buffers(U16, seq16=48, up16=128, ls=12, cmpz=6))
 SCRATCH.update(buffers(BF, qsb=768, rmb=768, cob=2048, scb=16, oneb=128, e2=128))
-SCRATCH.update(buffers(F32, onef=128, idn=128, sct=128, msk=128, iot=768, row=264, win0=1032, win1=1032, c1=512, c2=512,
+SCRATCH.update(buffers(F32, onef=128, idn=128, sct=128, msk=128, iot=768, row=264, win0=1032, win1=1032, c1=XA, c2=XA,
                        qp=264, rp=264, rps=96, rmp=512, mgz=96, keep=96, run=96, sp1=256, sp2=256, pr1=1032, pr2=1024,
-                       b1=264, b2=256, h1=512, h2=512, g3=96, cb0=776, cb1=776, cb2=776, ysb=768,
+                       b1=264, b2=256, x2=256, h1=1024 - XA, h2=1024 - XA, g3=96, cb0=776, cb1=776, cb2=776, ysb=192,
                        sb0=96, sb1=96, sb2=96, sb3=96, sb4=96, sb5=96))
 LOADS = ["seqi", "upi", "sndi", "qsb", "rmb", "co1", "co2", "scb"]
 SEMAPHORES = (["q_v", "q_a", "q_p", "q_g", "sent", "y0", "y1"] + ["ld_" + n for n in LOADS] + ["arr%d" % i for i in range(6)])
@@ -104,6 +105,9 @@ def rank_program(g, core, T, topo):
     def fill(x, v):
         emit("v", lambda: g.vector.memset(ap(x), v), [], [x])
 
+    def zeros(x):
+        emit("g", lambda: g.iota(ap(x), [[0, x[2] - x[1]]], 0, 0, allow_small_or_imprecise_dtypes=True), [], [x])
+
     def tt(out, a, b, op):
         emit("v", lambda: g.vector.tensor_tensor(ap(out), ap(a), ap(b), op), [a, b], [out])
 
@@ -133,9 +137,12 @@ def rank_program(g, core, T, topo):
 
     IDN = ("idn", 0, 128)
 
+    def scatter(w, cb, x, y, op):
+        o = ("seq16", 16 * w, 16 * w + 16)
+        emit("v", lambda: g.vector.tensor_tensor(ind((cb, 0, 768), o), ap(x), ap(y), op), [x, y, o], [(cb, 0, 768)])
+
     def scatter_sum(w, cb):
-        x, y, o = ("b%d" % w, 0, 256), ("pr%d" % w, 768, 1024), ("seq16", 16 * w, 16 * w + 16)
-        emit("v", lambda: g.vector.tensor_tensor(ind((cb, 0, 768), o), ap(x), ap(y), A.add), [x, y, o], [(cb, 0, 768)])
+        scatter(w, cb, ("b%d" % w, 0, 256), ("pr%d" % w, 768, 1024), A.add)
 
     def send(k, w):
         i = 2 * k + w
@@ -175,12 +182,12 @@ def rank_program(g, core, T, topo):
          [("oneb", 0, 128)], [("e2", 0, 128)])
     fill(("qp", 256, 264), 0.0)
     fill(("rp", 256, 264), 0.0)
-    for b in ("win0", "win1"):
-        fill((b, 256, SL), 0.0)
-        fill((b, 1024, 1032), 0.0)
+    for b, z in (("win0", lambda x: fill(x, 0.0)), ("win1", zeros)):
+        z((b, 256, SL))
+        z((b, 1024, 1032))
         for w in (0, 1):
             lo = SL + (w * len(cores) + rank) * 32
-            fill((b, lo, lo + 32), 0.0)
+            z((b, lo, lo + 32))
     fill(("row", 256, 264), 768.0)
     fill(("b1", 256, 264), 0.0)
     fill(("pr1", 1024, 1032), 0.0)
@@ -216,41 +223,50 @@ def rank_program(g, core, T, topo):
     emit("g", lambda: g.iota(T.iot[:, :], [[1, 768]], 0, 0, allow_small_or_imprecise_dtypes=True), [], [("iot", 0, 768)])
 
     RMP = [None, ("rmp", 0, 256), ("rmp", 256, 512)]
-    PRM = [None, ("ps_s1", 0, 256), ("ps_s2", 0, 256)]
+    PRM = [None, ("ps_s1", 0, 256), ("ps_y1", 256, 512)]
     RMC = [(("ps_y0", 0, 512), 0, 512), (("ps_y1", 0, 256), 512, 768)]
     for p, lo, hi in RMC:
         cpa(p, ("rmb", lo, hi))
-    for w in (1, 2):
-        ga(RMP[w], ("rmb", 0, 768), SEQ[w])
-        cpa(PRM[w], RMP[w])
+    ga(RMP[1], ("rmb", 0, 768), SEQ[1])
+    cpa(PRM[1], RMP[1])
     ts(("upt", 0, 64), ("upi", 0, 64), 1024.0, float(ZC - 1024), A.is_equal, A.mult)
     tt(("upz", 0, 64), ("upi", 0, 64), ("upt", 0, 64), A.add)
     cpv(("up16", 0, 64), ("upz", 0, 64))
     for p, lo, hi in RMC:
         tt(("cb0", lo, hi), ("qsb", lo, hi), p, A.mult)
     ga(("win0", 0, 256), ("cb0", 0, 768), SEQ[0])
-    for w in (1, 2):
-        ga(("sp%d" % w, 0, 256), ("cb0", 0, 768), SEQ[w])
+    ga(("sp1", 0, 256), ("cb0", 0, 768), SEQ[1])
 
-    def coef(w, us):
-        for u in us:
-            out = ("c%d" % w, 256 * u, 256 * u + 256) if u < 2 else ("ps_c%d" % w, 256 * u - 512, 256 * u - 256)
-            c = 1024 * (w - 1) + 256 * u
-            tt(out, ("cob", c, c + 256), PRM[w], A.mult)
+    def pc(w, i):
+        return ("ps_c%d" % w, 0, 1024 - XB) if i else ("ps_c3", 256 * w - 256, 256 * w - 256 + XB - XA)
+
+    def fold(w):
+        p, c = PRM[w], 1024 * (w - 1)
+        for lo, hi, out in ((0, 256, ("c%d" % w, 0)), (256, XA, ("c%d" % w, 256)), (XA, XB, pc(w, 0)), (XB, 1024, pc(w, 1))):
+            at = lo
+            while at < hi:
+                i = p[1] + at % 256
+                n = min(hi - at, p[2] - i)
+                o = out[1] + at - lo
+                tt((out[0], o, o + n), ("cob", c + at, c + at + n), (p[0], i, i + n), A.mult)
+                at += n
 
     def presum(w):
         mm(("ps_w", 0, 256), IDN, ("sp%d" % w, 0, 256), True, False)
 
     mm(("ps_s0", 0, 128), ("e2", 0, 128, 16), ("e2", 0, 128, 16), True, True)
     presum(1)
-    coef(1, (0, 1, 2, 3))
+    fold(1)
     snd_list(1)
-    coef(2, (0, 1, 2))
     cpv(("up16", 64, 128), ("upi", 64, 128))
 
     def flux(k, h):
-        lo, hi = YC[h]
-        mm(("ps_y%d" % h, 0, hi - lo, 16), ("msk", 0, 16), ("cb%d" % k, lo, hi), k == 0, k == SW - 1)
+        ps = "ps_y%d" % h
+        n = NJ // 2
+        if k == 0:
+            mm((ps, 0, 32 * n), ("win0", ZC, ZC + 128), ("idn", 0, 32 * n), True, False)
+        for i in range(n):
+            mm((ps, 32 * i, 32 * i + 32), ("cb%d" % k, n * h + i, 768, 128, NJ), ("msk", 0, 32), False, k == SW - 1 and i == n - 1)
 
     def spare(k):
         if k > 0:
@@ -261,41 +277,53 @@ def rank_program(g, core, T, topo):
         ga(("row", 0, 256), ("iot", 0, 768), SEQ[0])
         cpa(("msk", 0, 128), ("ps_s0", 0, 128))
         cpa(("sct", 0, 128), ("ps_s0", 128, 256))
+        cpa(PRM[2], RMP[2])
 
-    def products(w, b, end, k):
-        pr, h, ps = "pr%d" % w, ("h%d" % w, 0, 512), ("ps_w", 0, 256)
-        up = 64 * (w - 1)
-        ga(h, (b, 0, end), ("up16", up + 32, up + 64))
+    def products(w, b, end, k, plain=False):
+        pr, h = "pr%d" % w, "h%d" % w
+
+        def up(lo, hi):
+            return ("up16", 64 * (w - 1) + lo // 16, 64 * (w - 1) + hi // 16)
+
+        ga((h, 0, XB - XA), (b, 0, end), up(XA, XB))
+        ga((h, XB - XA, 1024 - XA), (b, 0, end), up(XB, 1024))
         for lo, hi in CUT:
-            gtt((pr, lo, hi), (b, 0, end), ("up16", up + lo // 16, up + hi // 16), ("c%d" % w, lo, hi))
-            mm(("ps_w", lo % 256, (hi - 1) % 256 + 1), IDN, (pr, lo, hi), False, hi == 512)
-        tt((pr, 512, 1024), h, ("ps_c%d" % w, 0, 512), A.mult)
+            c = ("cob", 1024 * (w - 1) + lo, 1024 * (w - 1) + hi) if plain else ("c%d" % w, lo, hi)
+            gtt((pr, lo, hi), (b, 0, end), up(lo, hi), c)
+            mm(("ps_w", lo % 256, (hi - 1) % 256 + 1), IDN, (pr, lo, hi), False, False)
+        tt((pr, XA, XB), (h, 0, XB - XA), pc(w, 0), A.mult)
+        mm(("ps_w", XA - 256, 256), IDN, (pr, XA, 512), False, True)
+        tt((pr, XB, 1024), (h, XB - XA, 1024 - XA), pc(w, 1), A.mult)
         if w == 1:
             ga(("g3", 0, 96), (pr, 768, 1025), LS[1])
+            cpa(("ps_s0", 256, 512), (pr, 768, 1024))
         else:
+            if plain:
+                cpa(("ps_s1", 0, 256), (pr, 768, 1024))
             spare(k)
-        tt(("b%d" % w, 0, 256), (pr, 512, 768), ps, A.add)
+        tt(("b%d" % w, 0, 256), (pr, 512, 768), ("ps_w", 0, 256), A.add)
 
     def wave1(k, b):
         products(1, b, 896, k)
         gtt(("sb%d" % (2 * k + 1), 0, 96), ("b1", 0, 257), LS[1], ("g3", 0, 96), A.add)
         send(k, 1)
-        tt((b, 256, 512), ("b1", 0, 256), ("pr1", 768, 1024), A.add)
-        presum(2)
-
-    def wave2(k, b, cb):
-        products(2, b, 1025, k)
-        scatter_sum(2, cb)
+        tt((b, 256, 512), ("b1", 0, 256), ("ps_s0", 256, 512), A.add)
 
     wave1(0, "win0")
+    ga(("sp2", 0, 256), ("qsb", 0, 768), SEQ[2])
+    ga(RMP[2], ("rmb", 0, 768), SEQ[2])
+    cpa(pc(2, 0), ("cob", 1024 + XA, 1024 + XB))
+    cpa(pc(2, 1), ("cob", 1024 + XB, 2048))
+    presum(2)
     scatter_sum(1, "cb0")
-    coef(2, (3,))
-    wave2(0, "win0", "cb0")
+    products(2, "win0", 1025, 0, True)
+    tt(("x2", 0, 256), ("b2", 0, 256), ("ps_s1", 0, 256), A.add)
+    scatter(2, "cb0", ("x2", 0, 256), RMP[2], A.mult)
 
     for k in range(1, SW):
         b, cb = "win%d" % (k % 2), "cb%d" % k
-        for i, (lo, hi) in enumerate(CH):
-            p = ("ps_s%d" % i, 0, hi - lo)
+        for i, (ps, at, lo, hi) in enumerate(CH):
+            p = (ps, at, at + hi - lo)
             mm(p, ("sct", 0, 128), ("cb%d" % (k - 1), lo, hi), True, True)
             if i == 0 and k == 1:
                 gtt(("mgz", 0, 96), ("row", 0, 257), LS[0], ("msk", 0, 96))
@@ -309,16 +337,25 @@ def rank_program(g, core, T, topo):
         for w in (1, 2):
             ga(("sp%d" % w, 0, 256), (cb, 0, 768), SEQ[w])
         presum(1)
+        if k == 1:
+            fold(2)
         wave1(k, b)
+        presum(2)
         flux(k - 1, 0)
         scatter_sum(1, cb)
-        wave2(k, b, cb)
+        products(2, b, 1025, k)
+        scatter_sum(2, cb)
 
-    for h, cp, q in ((0, cpv, "s"), (1, cpa, "a")):
+    n = NJ // 2
+    for h in range(2):
         flux(SW - 1, h)
-        lo, hi = YC[h]
-        x = ("ysb", lo, hi, 16)
-        cp(x, ("ps_y%d" % h, 0, hi - lo, 16))
-        emit(q, lambda: eng[q].dma_start(T.y[:, lo:hi], ap(x)), [x], [], sem="y%d" % h, n=16)
+        for i in range(n):
+            src, dst = ("ps_y%d" % h, 32 * i, 32 * i + 32), ("ysb", n * h + i, 32 * NJ, 128, NJ)
+            emit("v", lambda: g.vector.transpose(ap(dst), ap(src)), [src], [("piece%d" % (n * h + i), 0, 1)])
+    for a in range(4):
+        q = "sa"[a % 2]
+        lo, hi = 32 * NJ * a, 32 * NJ * (a + 1)
+        emit(q, lambda: eng[q].dma_start(T.y[:, lo:hi], T.ysb[32 * a:32 * a + 16, :]), [("piece%d" % j, 0, 1) for j in range(NJ)],
+             [], sem="y%d" % (a % 2), n=16)
     for s in ("q_v", "q_a", "q_p", "q_g", "y0", "y1", "sent"):
         g.wait_ge(T.sem[s], count[s])

from concourse.bass import DstId, RemoteDMATransfer
from concourse.mybir import AluOpType, ActivationFunctionType

SW = 3
ZC = 512
SL = 768
CUT = [(0, 96), (96, 256), (256, 448)]
XA, XB = 448, 640
CH = [("ps_s0", 0, 0, 416), ("ps_s1", 0, 416, 656), ("ps_w", 256, 656, 768)]
NJ = 6
F32, BF, I32, U16 = "float32", "bfloat16", "int32", "uint16"


def buffers(dtype, **cols):
    return {n: ("sbuf", [128, c], dtype) for n, c in cols.items()}


SCRATCH = {n: ("psum", [128, 512], F32) for n in ("ps_s0", "ps_s1", "ps_y0", "ps_y1", "ps_w", "ps_c1", "ps_c2", "ps_c3")}
SCRATCH.update(buffers(I32, seqi=48, upi=128, sndi=16, upt=64, upz=64))
SCRATCH.update(buffers(U16, seq16=48, up16=128, ls=12, cmpz=6))
SCRATCH.update(buffers(BF, qsb=768, rmb=768, cob=2048, scb=16, oneb=128, e2=128))
SCRATCH.update(buffers(F32, onef=128, idn=128, sct=128, msk=128, iot=768, row=264, win0=1032, win1=1032, c1=XA, c2=XA,
                       qp=264, rp=264, rps=96, rmp=512, mgz=96, keep=96, run=96, sp1=256, sp2=256, pr1=1032, pr2=1024,
                       b1=264, b2=256, x2=256, h1=1024 - XA, h2=1024 - XA, g3=96, cb0=776, cb1=776, cb2=776, ysb=192,
                       sb0=96, sb1=96, sb2=96, sb3=96, sb4=96, sb5=96))
LOADS = ["seqi", "upi", "sndi", "qsb", "rmb", "co1", "co2", "scb"]
SEMAPHORES = (["q_v", "q_a", "q_p", "q_g", "sent", "y0", "y1"] + ["ld_" + n for n in LOADS] + ["arr%d" % i for i in range(6)])


def plan(src, cores, topo):
    dst = [c for c in cores if c != src]
    far = [c for c in dst if topo.die(c) != topo.die(src)]
    near = [c for c in dst if topo.die(c) == topo.die(src)]
    return [[(d, topo.engines(src, d)[i::len(grp)]) for i, d in enumerate(grp)] for grp in (far, near) if grp]


def rank_program(g, core, T, topo):
    rank = T.rank_of(core)
    if rank is None:
        return
    A = AluOpType
    COPY = ActivationFunctionType.Copy
    cores = list(T.cores)
    others = [d for d in range(len(cores)) if d != rank]
    eng = {"v": g.vector, "a": g.scalar, "p": g.tensor, "g": g, "s": g.sync}

    count, hist, clock = {}, {}, {}
    known = {q: {} for q in eng}

    def need(q, tok):
        s, c = tok
        if known[q].get(s, 0) >= c:
            return
        eng[q].wait_ge(T.sem[s], c)
        for s2, c2 in clock.get(tok, {}).items():
            if known[q].get(s2, 0) < c2:
                known[q][s2] = c2
        known[q][s] = c

    def deps(q, reads, writes):
        toks = {}
        for lst, w in ((reads, True), (writes, False)):
            for x in lst:
                n, lo, hi = x[:3]
                psum = n[:3] == "ps_"
                for (l2, h2, kind, tok, q2) in hist.get(n, []):
                    if psum:
                        hit = q2 != q or (q != "p" and l2 < hi and lo < h2 and (kind == "w" or not w))
                    else:
                        hit = l2 < hi and lo < h2 and (kind == "w" or not w)
                    if hit and toks.get(tok[0], 0) < tok[1]:
                        toks[tok[0]] = tok[1]
        for s in sorted(toks, key=lambda s: -len(clock.get((s, toks[s]), {}))):
            need(q, (s, toks[s]))

    def note(q, reads, writes, tok):
        for lst, kind in ((reads, "r"), (writes, "w")):
            for x in lst:
                h = hist.setdefault(x[0], [])
                if kind == "w" and x[0][:3] != "ps_":
                    h[:] = [e for e in h if not (x[1] <= e[0] and e[1] <= x[2])]
                h.append((x[1], x[2], kind, tok, q))

    def emit(q, fn, reads, writes, sem=None, n=1):
        deps(q, reads, writes)
        s = sem or "q_" + q
        count[s] = count.get(s, 0) + n
        fn().then_inc(T.sem[s], n)
        tok = (s, count[s])
        c = dict(known[q])
        c[s] = count[s]
        clock[tok] = c
        note(q, reads, writes, tok)

    def ap(x):
        p = x[3] if len(x) > 3 else 128
        return T[x[0]][0:p, x[1]:x[2]] if len(x) < 5 else T[x[0]][0:p, x[1]:x[2]:x[4]]

    def ind(w, o):
        return T[w[0]][:, w[1]:w[2]].indirect(T[o[0]][:, o[1]:o[2]])

    def load(q, sem, dst, src_ap):
        emit(q, lambda: eng[q].dma_start(ap(dst), src_ap), [], [dst], sem="ld_" + sem, n=16)

    def fill(x, v):
        emit("v", lambda: g.vector.memset(ap(x), v), [], [x])

    def zeros(x):
        emit("g", lambda: g.iota(ap(x), [[0, x[2] - x[1]]], 0, 0, allow_small_or_imprecise_dtypes=True), [], [x])

    def tt(out, a, b, op):
        emit("v", lambda: g.vector.tensor_tensor(ap(out), ap(a), ap(b), op), [a, b], [out])

    def gtt(out, w, o, b, op=A.mult):
        emit("v", lambda: g.vector.tensor_tensor(ap(out), ind(w, o), ap(b), op), [w, o, b], [out])

    def gv(out, w, o):
        emit("v", lambda: g.vector.tensor_copy(ap(out), ind(w, o)), [w, o], [out])

    def ga(out, w, o):
        emit("a", lambda: g.scalar.activation(ap(out), ind(w, o), COPY), [w, o], [out])

    def cpv(out, a):
        emit("v", lambda: g.vector.tensor_copy(ap(out), ap(a)), [a], [out])

    def cpa(out, a):
        emit("a", lambda: g.scalar.activation(ap(out), ap(a), COPY), [a], [out])

    def ts(out, a, s1, s2, op0, op1=None):
        if op1 is None:
            emit("v", lambda: g.vector.tensor_scalar(ap(out), ap(a), s1, None, op0), [a], [out])
        else:
            emit("v", lambda: g.vector.tensor_scalar(ap(out), ap(a), s1, s2, op0, op1), [a], [out])

    def mm(out, l, r, start, stop):
        emit("p", lambda: g.tensor.matmul(ap(out), ap(l), ap(r), start, stop), [l, r], [out])

    IDN = ("idn", 0, 128)

    def scatter(w, cb, x, y, op):
        o = ("seq16", 16 * w, 16 * w + 16)
        emit("v", lambda: g.vector.tensor_tensor(ind((cb, 0, 768), o), ap(x), ap(y), op), [x, y, o], [(cb, 0, 768)])

    def scatter_sum(w, cb):
        scatter(w, cb, ("b%d" % w, 0, 256), ("pr%d" % w, 768, 1024), A.add)

    def send(k, w):
        i = 2 * k + w
        sb = "sb%d" % i
        deps("g", [(sb, 0, 96)], [])
        lo = SL + (w * len(cores) + rank) * 32
        for call in plan(core, cores, topo):
            tr = []
            for c, engines in call:
                j = others.index(cores.index(c))
                rid, pid = topo.addr(c)[:2]
                m = 0
                for e in engines:
                    m |= 1 << e
                tr.append(RemoteDMATransfer(dst_ids=[DstId(rid=rid, pnc=pid)], dma_engine_mask=m, remote_sem=T.sem["arr%d" % i],
                                            src=T[sb][:, 32 * j:32 * j + 32], dst=T["win%d" % (k % 2)][:, lo:lo + 32]))
                count["sent"] = count.get("sent", 0) + len(engines)
            g.remote_dma_fused(tr, local_sem=T.sem.sent)
        tot = sum(len(e) for d in others for call in plan(cores[d], cores, topo) for c, e in call if c == core)
        for d in others:
            a = SL + (w * len(cores) + d) * 32
            note("net", [], [("win%d" % (k % 2), a, a + 32)], ("arr%d" % i, tot))

    load("s", "seqi", ("seqi", 0, 48), T.seq[:, :])
    load("a", "rmb", ("rmb", 0, 768), T.rm[:, :])
    load("s", "qsb", ("qsb", 0, 768), T.qs[:, :])
    load("a", "sndi", ("sndi", 0, 16), T.snd[:, :])
    load("s", "upi", ("upi", 0, 128), T.up[:, 64:192])
    load("s", "co1", ("cob", 0, 1024), T.co[:, 1024:2048])
    load("a", "co2", ("cob", 1024, 2048), T.co[:, 2048:3072])
    load("s", "scb", ("scb", 0, 16, 16), T.sc[:, :])

    fill(("onef", 0, 128), 1.0)
    fill(("oneb", 0, 128, 16), 1.0)
    emit("g", lambda: g.affine_select(T.idn[:, :], T.onef[:, :], [[-1, 128]], A.is_equal, 0.0, 0, 1), [("onef", 0, 128)], [IDN])
    emit("g", lambda: g.affine_select(T.e2[0:16, :], T.oneb[0:16, :], [[0, 8], [1, 16]], A.is_equal, 0.0, 0, -1),
         [("oneb", 0, 128)], [("e2", 0, 128)])
    fill(("qp", 256, 264), 0.0)
    fill(("rp", 256, 264), 0.0)
    for b, z in (("win0", lambda x: fill(x, 0.0)), ("win1", zeros)):
        z((b, 256, SL))
        z((b, 1024, 1032))
        for w in (0, 1):
            lo = SL + (w * len(cores) + rank) * 32
            z((b, lo, lo + 32))
    fill(("row", 256, 264), 768.0)
    fill(("b1", 256, 264), 0.0)
    fill(("pr1", 1024, 1032), 0.0)
    fill(("cb1", 768, 776), 0.0)
    fill(("cb2", 768, 776), 0.0)
    fill(("keep", 0, 96), 1.0)
    fill(("keep", 0, 96, 128, 16), 0.0)

    SEQ = [("seq16", 16 * w, 16 * w + 16) for w in range(3)]
    LS = [("ls", 0, 6), ("ls", 6, 12)]
    cpv(("seq16", 0, 48), ("seqi", 0, 48))

    def snd_list(w):
        j = 0
        while j < 3:
            n = 1
            while j + n < 3 and others[j + n] == others[j] + n:
                n += 1
            a = 8 * w + 2 * others[j]
            o, x = ("ls", 6 * w + 2 * j, 6 * w + 2 * (j + n)), ("sndi", a, a + 2 * n)
            if w:
                ts(o, x, 512.0, -256.0, A.min, A.add)
            else:
                ts(o, x, 256.0, None, A.min)
            j += n

    ga(("rp", 0, 256), ("rmb", 0, 768), SEQ[0])
    snd_list(0)
    ga(("rps", 0, 96), ("rp", 0, 257), LS[0])
    gv(("qp", 0, 256), ("qsb", 0, 768), SEQ[0])
    gtt(("sb0", 0, 96), ("qp", 0, 257), LS[0], ("rps", 0, 96))
    send(0, 0)
    emit("g", lambda: g.iota(T.iot[:, :], [[1, 768]], 0, 0, allow_small_or_imprecise_dtypes=True), [], [("iot", 0, 768)])

    RMP = [None, ("rmp", 0, 256), ("rmp", 256, 512)]
    PRM = [None, ("ps_s1", 0, 256), ("ps_y1", 256, 512)]
    RMC = [(("ps_y0", 0, 512), 0, 512), (("ps_y1", 0, 256), 512, 768)]
    for p, lo, hi in RMC:
        cpa(p, ("rmb", lo, hi))
    ga(RMP[1], ("rmb", 0, 768), SEQ[1])
    cpa(PRM[1], RMP[1])
    ts(("upt", 0, 64), ("upi", 0, 64), 1024.0, float(ZC - 1024), A.is_equal, A.mult)
    tt(("upz", 0, 64), ("upi", 0, 64), ("upt", 0, 64), A.add)
    cpv(("up16", 0, 64), ("upz", 0, 64))
    for p, lo, hi in RMC:
        tt(("cb0", lo, hi), ("qsb", lo, hi), p, A.mult)
    ga(("win0", 0, 256), ("cb0", 0, 768), SEQ[0])
    ga(("sp1", 0, 256), ("cb0", 0, 768), SEQ[1])

    def pc(w, i):
        return ("ps_c%d" % w, 0, 1024 - XB) if i else ("ps_c3", 256 * w - 256, 256 * w - 256 + XB - XA)

    def fold(w):
        p, c = PRM[w], 1024 * (w - 1)
        for lo, hi, out in ((0, 256, ("c%d" % w, 0)), (256, XA, ("c%d" % w, 256)), (XA, XB, pc(w, 0)), (XB, 1024, pc(w, 1))):
            at = lo
            while at < hi:
                i = p[1] + at % 256
                n = min(hi - at, p[2] - i)
                o = out[1] + at - lo
                tt((out[0], o, o + n), ("cob", c + at, c + at + n), (p[0], i, i + n), A.mult)
                at += n

    def presum(w):
        mm(("ps_w", 0, 256), IDN, ("sp%d" % w, 0, 256), True, False)

    mm(("ps_s0", 0, 128), ("e2", 0, 128, 16), ("e2", 0, 128, 16), True, True)
    presum(1)
    fold(1)
    snd_list(1)
    cpv(("up16", 64, 128), ("upi", 64, 128))

    def flux(k, h):
        ps = "ps_y%d" % h
        n = NJ // 2
        if k == 0:
            mm((ps, 0, 32 * n), ("win0", ZC, ZC + 128), ("idn", 0, 32 * n), True, False)
        for i in range(n):
            mm((ps, 32 * i, 32 * i + 32), ("cb%d" % k, n * h + i, 768, 128, NJ), ("msk", 0, 32), False, k == SW - 1 and i == n - 1)

    def spare(k):
        if k > 0:
            flux(k - 1, 1)
            return
        for o in range(8):
            mm(("ps_s0", 128 + 16 * o, 144 + 16 * o), ("e2", 0, 128, 16), ("scb", 0, 16, 16), True, True)
        ga(("row", 0, 256), ("iot", 0, 768), SEQ[0])
        cpa(("msk", 0, 128), ("ps_s0", 0, 128))
        cpa(("sct", 0, 128), ("ps_s0", 128, 256))
        cpa(PRM[2], RMP[2])

    def products(w, b, end, k, plain=False):
        pr, h = "pr%d" % w, "h%d" % w

        def up(lo, hi):
            return ("up16", 64 * (w - 1) + lo // 16, 64 * (w - 1) + hi // 16)

        ga((h, 0, XB - XA), (b, 0, end), up(XA, XB))
        ga((h, XB - XA, 1024 - XA), (b, 0, end), up(XB, 1024))
        for lo, hi in CUT:
            c = ("cob", 1024 * (w - 1) + lo, 1024 * (w - 1) + hi) if plain else ("c%d" % w, lo, hi)
            gtt((pr, lo, hi), (b, 0, end), up(lo, hi), c)
            mm(("ps_w", lo % 256, (hi - 1) % 256 + 1), IDN, (pr, lo, hi), False, False)
        tt((pr, XA, XB), (h, 0, XB - XA), pc(w, 0), A.mult)
        mm(("ps_w", XA - 256, 256), IDN, (pr, XA, 512), False, True)
        tt((pr, XB, 1024), (h, XB - XA, 1024 - XA), pc(w, 1), A.mult)
        if w == 1:
            ga(("g3", 0, 96), (pr, 768, 1025), LS[1])
            cpa(("ps_s0", 256, 512), (pr, 768, 1024))
        else:
            if plain:
                cpa(("ps_s1", 0, 256), (pr, 768, 1024))
            spare(k)
        tt(("b%d" % w, 0, 256), (pr, 512, 768), ("ps_w", 0, 256), A.add)

    def wave1(k, b):
        products(1, b, 896, k)
        gtt(("sb%d" % (2 * k + 1), 0, 96), ("b1", 0, 257), LS[1], ("g3", 0, 96), A.add)
        send(k, 1)
        tt((b, 256, 512), ("b1", 0, 256), ("ps_s0", 256, 512), A.add)

    wave1(0, "win0")
    ga(("sp2", 0, 256), ("qsb", 0, 768), SEQ[2])
    ga(RMP[2], ("rmb", 0, 768), SEQ[2])
    cpa(pc(2, 0), ("cob", 1024 + XA, 1024 + XB))
    cpa(pc(2, 1), ("cob", 1024 + XB, 2048))
    presum(2)
    scatter_sum(1, "cb0")
    products(2, "win0", 1025, 0, True)
    tt(("x2", 0, 256), ("b2", 0, 256), ("ps_s1", 0, 256), A.add)
    scatter(2, "cb0", ("x2", 0, 256), RMP[2], A.mult)

    for k in range(1, SW):
        b, cb = "win%d" % (k % 2), "cb%d" % k
        for i, (ps, at, lo, hi) in enumerate(CH):
            p = (ps, at, at + hi - lo)
            mm(p, ("sct", 0, 128), ("cb%d" % (k - 1), lo, hi), True, True)
            if i == 0 and k == 1:
                gtt(("mgz", 0, 96), ("row", 0, 257), LS[0], ("msk", 0, 96))
                r, m, x = ("run", 0, 96), ("keep", 0, 96), ("mgz", 0, 96)
                emit("v", lambda: g.vector.tensor_tensor_scan(ap(r), ap(m), ap(x), 0.0, A.mult, A.add), [m, x], [r])
                cpv(("cmpz", 0, 6), ("run", 15, 96, 128, 16))
            tt((cb, lo, hi), p, ("rmb", lo, hi), A.mult)
        gv(("sb%d" % (2 * k), 0, 96), (cb, 0, 769), ("cmpz", 0, 6))
        send(k, 0)
        gv((b, 0, 256), (cb, 0, 768), SEQ[0])
        for w in (1, 2):
            ga(("sp%d" % w, 0, 256), (cb, 0, 768), SEQ[w])
        presum(1)
        if k == 1:
            fold(2)
        wave1(k, b)
        presum(2)
        flux(k - 1, 0)
        scatter_sum(1, cb)
        products(2, b, 1025, k)
        scatter_sum(2, cb)

    n = NJ // 2
    for h in range(2):
        flux(SW - 1, h)
        for i in range(n):
            src, dst = ("ps_y%d" % h, 32 * i, 32 * i + 32), ("ysb", n * h + i, 32 * NJ, 128, NJ)
            emit("v", lambda: g.vector.transpose(ap(dst), ap(src)), [src], [("piece%d" % (n * h + i), 0, 1)])
    for a in range(4):
        q = "sa"[a % 2]
        lo, hi = 32 * NJ * a, 32 * NJ * (a + 1)
        emit(q, lambda: eng[q].dma_start(T.y[:, lo:hi], T.ysb[32 * a:32 * a + 16, :]), [("piece%d" % j, 0, 1) for j in range(NJ)],
             [], sem="y%d" % (a % 2), n=16)
    for s in ("q_v", "q_a", "q_p", "q_g", "y0", "y1", "sent"):
        g.wait_ge(T.sem[s], count[s])
